import numpy as np
import ml_dtypes


def mxq(x, axis, fmt="e4m3"):
    dtype, down = {"e4m3": (ml_dtypes.float8_e4m3fn, 7), "e5m2": (ml_dtypes.float8_e5m2, 14)}[fmt]
    v = np.moveaxis(np.asarray(x, np.float32).astype(ml_dtypes.bfloat16).astype(np.float64), axis, -1)
    blocks = v.reshape(v.shape[:-1] + (-1, 32))
    amax = np.abs(blocks).max(-1, keepdims=True)
    byte = np.maximum(np.where(amax > 0, np.frexp(amax)[1] - 1 + 127, 0) - down, 1)
    scale = np.exp2(byte - 127.0)
    codes = (blocks / scale).astype(np.float32).astype(dtype).astype(np.float64)
    return np.moveaxis((codes * scale).reshape(v.shape), -1, axis)


WIDE = False


def mx_kscale(k):
    if not WIDE:
        return np.ones(k)
    levels = np.array([10, -10, 5, -5, 0])
    if k % 512:
        return np.exp2(np.random.permutation(np.resize(levels, k // 32))).repeat(32)
    a = np.empty((k // 512, 16))
    for p in range(k // 512):
        a[p, :8] = np.random.permutation(np.resize(levels, 8))
        for g in range(8):
            far = levels[np.abs(levels - a[p, g]) >= 10]
            a[p, g + 8] = far[np.random.randint(len(far))]
    return np.exp2(a.ravel()).repeat(32)


BF16 = ml_dtypes.bfloat16


def bf(x):
    return np.asarray(x, np.float32).astype(BF16)


def f64(x):
    return np.asarray(x).astype(np.float64)


E2M1 = np.array([0.0, 0.5, 1.0, 1.5, 2.0, 3.0, 4.0, 6.0, -0.0, -0.5, -1.0, -1.5, -2.0, -3.0, -4.0, -6.0])


def pack_weight(w, fmt):
    k, n = w.shape
    w = f64(bf(w)).reshape(k // 32, 32, n)
    amax = np.abs(w).max(1)
    if fmt == "e4m3":
        byte = np.frexp(amax)[1] - 1 + 127 - 7
    else:
        mant, ex = np.frexp(amax / 6.0)
        byte = np.where(mant > 0.5, ex, ex - 1) + 127
    byte = np.clip(np.where(amax > 0, byte, 1), 1, 254)
    scaled = (w * np.exp2(127.0 - byte)[:, None, :]).reshape(k, n).astype(np.float32)
    by_word = np.ascontiguousarray(scaled.reshape(k // 512, 128, 4, n).transpose(0, 1, 3, 2))
    if fmt == "e4m3":
        words = by_word.astype(ml_dtypes.float8_e4m3fn).view(np.uint8)
    else:
        c = by_word.astype(ml_dtypes.float4_e2m1fn).view(np.uint8) & 0xF
        words = c[..., 0::2] | (c[..., 1::2] << 4)
    return np.ascontiguousarray(words), np.ascontiguousarray(byte.astype(np.uint8).reshape(k // 512, 16, n))


def unpack_weight(words, scales, fmt):
    g, p, n, _ = words.shape
    if fmt == "e4m3":
        vals = np.ascontiguousarray(words).view(ml_dtypes.float8_e4m3fn).astype(np.float64)
    else:
        nib = np.empty((g, p, n, 4), np.uint8)
        nib[..., 0::2] = words & 0xF
        nib[..., 1::2] = words >> 4
        vals = E2M1[nib]
    vals = vals * np.repeat(np.exp2(scales.astype(np.float64) - 127.0), 8, axis=1)[..., None]
    return vals.transpose(0, 1, 3, 2).reshape(g * 512, n)
def pack4(w):
    words, scales = pack_weight(w, "e2m1")
    return words.reshape(words.shape[0], 128, -1), scales


def unpack4(words, scales):
    return unpack_weight(words.reshape(words.shape[0], 128, -1, 2), scales, "e2m1")


def planes(Y):
    n, m = Y.shape
    b = f64(bf(Y)).reshape(n // 32, 32, m)
    amax = np.abs(b).max(1)
    byte = np.clip(np.where(amax > 0, np.frexp(amax)[1] - 1 + 127 - 7, 1), 1, 254)
    codes = (b * np.exp2(127.0 - byte)[:, None, :]).reshape(n, m).astype(np.float32).astype(ml_dtypes.float8_e4m3fn).view(np.uint8)
    words = codes.reshape(n // 512, 128, 4, m).transpose(0, 1, 3, 2)
    return np.ascontiguousarray(words), np.ascontiguousarray(byte.astype(np.uint8).reshape(n // 512, 16, m))


S, C, F, B = 2048, 512, 1024, 1536

def setup_inputs():
    s = mx_kscale(C)
    t = mx_kscale(F)
    R = np.random.randn(S, C) * np.exp(0.4 * np.random.randn(S, 1))
    W = (0.8 * np.random.randn(C, F) + 0.6 * np.random.randn(C, 1)) / np.sqrt(C)
    P = np.exp(1.2 * np.random.randn(F, B)) / F
    criterion_words, criterion_scales = pack4(W / s[:, None])
    spend_words, spend_scales = pack4(P / t[:, None])
    return {
        "ratings": bf(R * s[None, :]),
        "criterion_words": criterion_words,
        "criterion_scales": criterion_scales,
        "loss_coef": bf(np.exp(0.5 * np.random.randn(F)) * t),
        "spend_words": spend_words,
        "spend_scales": spend_scales,
        "priorities": bf(np.exp(0.8 * np.random.randn(B))),
    }

def reference(ratings, criterion_words, criterion_scales, loss_coef, spend_words, spend_scales, priorities):
    W = unpack4(criterion_words, criterion_scales)
    P = unpack4(spend_words, spend_scales)
    A = mxq(f64(ratings), 1, "e4m3") @ W
    H = np.square(A) * f64(loss_coef)[None, :]
    Z = mxq(H, 1, "e4m3") @ P
    y = np.log(1.0 + Z) * f64(priorities)[None, :]
    Y = y.T
    words, scales = planes(Y)
    return y, words, scales

@@ -1,0 +1,386 @@
+from contextlib import ExitStack
+
+import concourse.mybir as mybir
+from concourse.masks import make_identity
+
+S, C, F, B = 2048, 512, 1024, 1536
+FLOPS = 2 * S * C * F + 2 * S * F * B
+
+F32 = mybir.dt.float32
+BF16 = mybir.dt.bfloat16
+I32 = mybir.dt.int32
+U32 = mybir.dt.uint32
+U8 = mybir.dt.uint8
+FP8X4 = mybir.dt.float8_e4m3fn_x4
+FP4X4 = mybir.dt.float4_e2m1fn_x4
+ACT = mybir.ActivationFunctionType
+ALU = mybir.AluOpType
+
+P = 128
+KP = 512
+TILES = S // P
+FG = F // KP
+BG = B // KP
+RING = 6
+HALF = B // 2
+PIECES = (0, 256, 768, 1536)
+LAST_PIECES = (0, 512, 768, 1024, 1536)
+R_LOADS = (2, 2, 4, 4, 4)
+WORD_STORES = (4, 4, 4, 1, 1, 1, 1)
+SCALE_STORES = (4, 4, 4, 3, 1)
+
+
+def runs(sizes):
+    table = {}
+    first = 0
+    for number, size in enumerate(sizes):
+        for i in range(first, first + size):
+            table[i] = (number, first, size)
+        first += size
+    return table
+
+
+def tile_supplier_quadratic_loss_h1_kernel(
+    tc, ratings, criterion_words, criterion_scales, loss_coef, spend_words, spend_scales, priorities, out_0, out_1, out_2
+):
+    nc = tc.nc
+    with ExitStack() as ctx:
+        keep = ctx.enter_context(tc.tile_pool(name="keep", bufs=1))
+        work = ctx.enter_context(tc.tile_pool(name="work", bufs=3))
+        psum = ctx.enter_context(tc.psum_pool(name="psum", bufs=1))
+        ctx.enter_context(tc.manual_schedule())
+
+        w_raw = keep.tile([P, 2 * F], U8, align_bytes=64)
+        w_scale_raw = keep.tile([P, F], U8, align_bytes=64)
+        w_codes = keep.tile([P, 2 * F], U8, align_bytes=64)
+        w_scales = keep.tile([P, F], U8, align_bytes=64)
+        p_codes = keep.tile([P, FG, 2 * B], U8, align_bytes=64)
+        p_scales = keep.tile([P, FG, B], U8, align_bytes=64)
+        rows = keep.tile([P, KP], BF16, align_bytes=64)
+        b_cols = keep.tile([P, 3, 4], BF16, align_bytes=64)
+        ident_f32 = keep.tile([P, P], F32, align_bytes=64)
+        ident_bf16 = keep.tile([P, P], BF16, align_bytes=64)
+        warm = keep.tile([P, 1], F32)
+        const_a = psum.tile([P, 2 * KP], BF16, tag="const_a")
+        const_b = psum.tile([P, 2 * KP], BF16, tag="const_b")
+
+        nc.vector.memset(w_scale_raw[:].bitcast(I32), 0)
+        nc.vector.memset(rows[:], 0.0)
+        make_identity(nc, ident_f32[:])
+        nc.gpsimd.dma_start(out=rows[0:FG, :], in_=loss_coef.rearrange("(g n) -> g n", g=FG))
+        nc.gpsimd.dma_start(out=rows[4:8, 0:384], in_=priorities.rearrange("(r n) -> r n", r=4))
+        nc.vector.tensor_copy(out=ident_bf16[:], in_=ident_f32[:])
+        nc.vector.memset(p_scales[:].rearrange("p g n -> p (g n)").bitcast(I32), 0)
+        nc.scalar.activation(out=warm[:], in_=ident_f32[:, 0:1], func=ACT.Ln, bias=1.0)
+
+        r_run = runs(R_LOADS)
+        r_tiles = {}
+
+        def load_ratings(number):
+            first = sum(R_LOADS[:number])
+            size = R_LOADS[number]
+            r_tiles[number] = keep.tile([P, size, C], BF16, name="r_in%d" % number, align_bytes=64)
+            nc.sync.dma_start(
+                out=r_tiles[number][:],
+                in_=ratings[first * P : (first + size) * P, :].rearrange("(j p) c -> p j c", p=P),
+            )
+
+        def load_w_words(g):
+            cols = slice(2 * KP * g, 2 * KP * (g + 1))
+            nc.sync.dma_start(out=w_raw[:, cols].bitcast(I32), in_=criterion_words[0, :, cols].bitcast(I32))
+
+        load_w_words(0)
+        load_ratings(0)
+        for q in range(4):
+            nc.sync.dma_start(
+                out=w_scale_raw[32 * q : 32 * q + 4, :].bitcast(I32),
+                in_=criterion_scales[0, 4 * q : 4 * q + 4, :].bitcast(I32),
+            )
+        load_w_words(1)
+        load_ratings(1)
+        nc.sync.dma_start(out=p_codes[:, 0, :].bitcast(I32), in_=spend_words[0].bitcast(I32))
+        for q in range(4):
+            nc.sync.dma_start(
+                out=p_scales[32 * q : 32 * q + 4, :, :].bitcast(I32),
+                in_=spend_scales[:, 4 * q : 4 * q + 4, :].rearrange("g r n -> r g n").bitcast(I32),
+            )
+        nc.sync.dma_start(out=p_codes[:, 1, :].bitcast(I32), in_=spend_words[1].bitcast(I32))
+        for number in range(2, len(R_LOADS)):
+            load_ratings(number)
+
+        def order_w_columns(g):
+            nc.vector.tensor_copy(
+                out=w_codes[:, 2 * KP * g : 2 * KP * (g + 1)].rearrange("p (t m b) -> p t m b", t=4, b=2),
+                in_=w_raw[:, 2 * KP * g : 2 * KP * (g + 1)].rearrange("p (m t b) -> p t m b", t=4, b=2),
+            )
+            nc.vector.tensor_copy(
+                out=w_scales[:, KP * g : KP * (g + 1)].rearrange("p (t m) -> p t m", t=4),
+                in_=w_scale_raw[:, KP * g : KP * (g + 1)].rearrange("p (m t) -> p t m", t=4),
+            )
+
+        banks_used = []
+
+        def next_bank():
+            tag = "bank%d" % (len(banks_used) % RING)
+            banks_used.append(tag)
+            return psum.tile([P, KP], F32, name=tag, tag=tag)
+
+        word_run = runs(WORD_STORES)
+        scale_run = runs(SCALE_STORES)
+        word_tiles = {}
+        scale_tiles = {}
+        r_q, squares, h_q, logs, y_bf16, turned = {}, {}, {}, {}, {}, {}
+
+        def live(i):
+            return 0 <= i < TILES
+
+        r_turned, y_turned = {}, {}
+
+        def transpose_ratings(bank, half, i):
+            number, first, size = r_run[i]
+            r_words = r_tiles[number][:, i - first, :].bitcast(F32)
+            for u in range(2):
+                col = P * (2 * half + u)
+                nc.tensor.transpose(bank[:, col : col + P], r_words[:, u : 2 * P : 2], ident_f32[:])
+
+        def transpose_result(bank, half, i, g):
+            y_words = y_bf16[i][:].bitcast(F32)
+            for u in range(2):
+                col = P * (2 * half + u)
+                first = u * (B // 4) + P * g
+                nc.tensor.transpose(bank[:, col : col + P], y_words[:, first : first + P], ident_f32[:])
+
+        def halves(bank):
+            return bank[:].rearrange("p (h u s) -> p h s u", h=2, u=2)
+
+        def as_bf16(words):
+            return words.rearrange("p s u -> p (s u)").bitcast(BF16)
+
+        def turn_ratings(tiles, copy):
+            slots = work.tile([P, len(tiles), P, 2], F32, tag="r_turned", name="r_turned", align_bytes=64)
+            bank = next_bank()
+            for half, i in enumerate(tiles):
+                transpose_ratings(bank, half, i)
+                r_turned[i] = as_bf16(slots[:, half])
+            copy(out=slots[:], in_=halves(bank)[:, 0 : len(tiles)])
+
+        def turn(y_tile, r_tile, copy_last):
+            slots = work.tile([P, 4, P, 2], F32, tag="turned", name="turned", align_bytes=64)
+            y_turned[y_tile] = [as_bf16(slots[:, g]) for g in range(BG)]
+            bank_x = next_bank()
+            transpose_result(bank_x, 0, y_tile, 0)
+            transpose_result(bank_x, 1, y_tile, 1)
+            bank_y = next_bank()
+            transpose_result(bank_y, 0, y_tile, 2)
+            used = 1
+            if live(r_tile):
+                transpose_ratings(bank_y, 1, r_tile)
+                r_turned[r_tile] = as_bf16(slots[:, 3])
+                used = 2
+            nc.scalar.copy(out=slots[:, 0:2], in_=halves(bank_x))
+            copy_last(out=slots[:, 2 : 2 + used], in_=halves(bank_y)[:, 0:used])
+
+        def score(i):
+            codes, scales = r_q[i]
+            squares[i] = work.tile([P, FG, P, 4], F32, tag="squares", name="squares", bufs=3, align_bytes=64)
+            for g in range(FG):
+                bank = next_bank()
+                for t in range(4):
+                    col = KP * g + P * t
+                    nc.tensor.matmul_mx(
+                        out=bank[:, P * t : P * (t + 1)],
+                        lhsT=w_codes[:, 2 * col : 2 * (col + P)].bitcast(FP4X4),
+                        lhsT_scale=w_scales[:, col : col + P],
+                        rhs=codes[:].bitcast(FP8X4),
+                        rhs_scale=scales[:],
+                        start=True,
+                        stop=True,
+                    )
+                nc.scalar.activation(
+                    out=squares[i][:, g], in_=bank[:].rearrange("p (t s) -> p s t", t=4), func=ACT.Square
+                )
+
+        def spend(i):
+            codes, scales = h_q[i]
+            logs[i] = work.tile([P, B], F32, tag="logs", name="logs", bufs=3, align_bytes=64)
+            for n in range(BG):
+                bank = next_bank()
+                for g in range(FG):
+                    nc.tensor.matmul_mx(
+                        out=bank[:],
+                        lhsT=codes[:, P * g : P * (g + 1)].bitcast(FP8X4),
+                        lhsT_scale=scales[:, P * g : P * (g + 1)],
+                        rhs=p_codes[:, g, 2 * KP * n : 2 * KP * (n + 1)].bitcast(FP4X4),
+                        rhs_scale=p_scales[:, g, KP * n : KP * (n + 1)],
+                        start=(g == 0),
+                        stop=(g == FG - 1),
+                    )
+                nc.scalar.activation(out=logs[i][:, KP * n : KP * (n + 1)], in_=bank[:], func=ACT.Ln, bias=1.0)
+
+        def b_row(lo, hi):
+            return const_a[:, lo:hi] if hi <= HALF else const_b[:, lo - HALF : hi - HALF]
+
+        c_view = (
+            const_a[:, HALF : HALF + 4 * FG].rearrange("p (t g) -> p g t", t=4).unsqueeze(2).to_broadcast([P, FG, P, 4])
+        )
+
+        y_f32 = {}
+
+        def cast_views(i, lo, hi):
+            out = y_bf16[i][:].rearrange("p (u m e) -> p u m e", u=2, e=2)[:, :, lo // 4 : hi // 4]
+            return out, y_f32[i][:, lo:hi].rearrange("p (m u e) -> p u m e", u=2, e=2)
+
+        def cast_on_gpsimd(i, lo, hi):
+            out, in_ = cast_views(i, lo, hi)
+            nc.gpsimd.tensor_scalar(out=out, in0=in_, scalar1=1.0, scalar2=1.0, op0=ALU.mult, op1=ALU.mult)
+
+        def cast_on_vector(i, lo, hi):
+            out, in_ = cast_views(i, lo, hi)
+            nc.vector.tensor_copy(out=out, in_=in_)
+
+        def cast_on_scalar(i, lo, hi):
+            out, in_ = cast_views(i, lo, hi)
+            nc.scalar.copy(out=out, in_=in_)
+
+        def new_result(i):
+            y_f32[i] = work.tile([P, B], F32, tag="y", name="y", bufs=4, align_bytes=64)
+            y_bf16[i] = work.tile([P, B], BF16, tag="y_bf16", name="y_bf16", align_bytes=64)
+
+        def weigh_piece(i, lo, hi):
+            nc.vector.tensor_tensor(out=y_f32[i][:, lo:hi], in0=logs[i][:, lo:hi], in1=b_row(lo, hi), op=ALU.mult)
+
+        def store_result(i, lo, hi):
+            nc.sync.dma_start(out=out_0[P * i : P * (i + 1), lo:hi], in_=y_f32[i][:, lo:hi])
+
+        def weigh(i, gpsimd_pieces):
+            new_result(i)
+            for n in range(3):
+                weigh_piece(i, PIECES[n], PIECES[n + 1])
+                if n < gpsimd_pieces:
+                    cast_on_gpsimd(i, PIECES[n], PIECES[n + 1])
+            store_result(i, 0, B)
+
+        h_bf16 = {}
+
+        def loss(i):
+            h_bf16[i] = work.tile([P, FG, P, 4], BF16, tag="h_bf16", name="h_bf16", align_bytes=64)
+            nc.vector.tensor_tensor(out=h_bf16[i][:], in0=squares[i][:], in1=c_view, op=ALU.mult)
+
+        def quantize_ratings(i):
+            codes = work.tile([P, P], U32, tag="r_codes", name="r_codes", bufs=4, align_bytes=64)
+            scales = work.tile([P, P], U8, tag="r_scales", name="r_scales", bufs=4, align_bytes=64)
+            r_q[i] = (codes, scales)
+            nc.vector.quantize_mx(out=codes[:].bitcast(FP8X4), scales=scales[:], in_=r_turned[i])
+
+        def quantize_loss(i):
+            codes = work.tile([P, FG * P], U32, tag="h_codes", name="h_codes", align_bytes=64)
+            scales = work.tile([P, FG * P], U8, tag="h_scales", name="h_scales", align_bytes=64)
+            h_q[i] = (codes, scales)
+            nc.vector.quantize_mx(
+                out=codes[:].bitcast(FP8X4), scales=scales[:], in_=h_bf16[i][:].rearrange("p g s t -> p (g s t)")
+            )
+
+        def quantize_result(i):
+            w_number, w_first, w_size = word_run[i]
+            s_number, s_first, s_size = scale_run[i]
+            if i == w_first:
+                word_tiles[w_number] = keep.tile([P, BG, w_size * P], U32, name="y_words%d" % w_number, align_bytes=64)
+            if i == s_first:
+                scale_tiles[s_number] = keep.tile([P, BG, s_size * P], U8, name="y_scales%d" % s_number, align_bytes=64)
+            words = word_tiles[w_number]
+            scales = scale_tiles[s_number]
+            for g in range(BG):
+                nc.vector.quantize_mx(
+                    out=words[:, g, P * (i - w_first) : P * (i - w_first + 1)].bitcast(FP8X4),
+                    scales=scales[:, g, P * (i - s_first) : P * (i - s_first + 1)],
+                    in_=y_turned[i][g],
+                )
+            if i == w_first + w_size - 1:
+                nc.sync.dma_start(
+                    out=out_1.rearrange("g p m t -> p g (m t)")[:, :, 4 * P * w_first : 4 * P * (i + 1)].bitcast(I32),
+                    in_=words[:].bitcast(I32),
+                )
+            if i == s_first + s_size - 1:
+                for q in range(4):
+                    nc.sync.dma_start(
+                        out=out_2[:, 4 * q : 4 * q + 4, P * s_first : P * (i + 1)]
+                        .rearrange("g r m -> r g m")
+                        .bitcast(I32),
+                        in_=scales[32 * q : 32 * q + 4, :, :].bitcast(I32),
+                    )
+
+        def turn_vectors():
+            for t in range(4):
+                nc.tensor.transpose(const_a[:, HALF + FG * t : HALF + FG * t + P], rows[:, t:KP:4], ident_bf16[:])
+            for m in range(3):
+                nc.tensor.transpose(const_b[:, P * m : P * (m + 1)], rows[:, P * m : P * (m + 1)], ident_bf16[:])
+            nc.vector.tensor_copy(out=b_cols[:], in_=const_b[:, 0 : 3 * P].rearrange("p (m r) -> p m r", m=3)[:, :, 4:8])
+
+        def spread_priorities(blocks):
+            for block in blocks:
+                r, m = divmod(block, 3)
+                nc.tensor.transpose(
+                    b_row(P * block, P * (block + 1)),
+                    b_cols[:, m, r : r + 1].to_broadcast([P, P]),
+                    ident_bf16[:],
+                )
+
+        order_w_columns(0)
+        turn_ratings([0], nc.scalar.copy)
+        turn_ratings([1], nc.scalar.copy)
+        turn_ratings([2, 3], nc.scalar.copy)
+        quantize_ratings(0)
+        order_w_columns(1)
+        quantize_ratings(1)
+        quantize_ratings(2)
+        quantize_ratings(3)
+        score(0)
+        score(1)
+        turn_vectors()
+        loss(0)
+        score(2)
+        spread_priorities(range(6, 12))
+        spread_priorities(range(6))
+        quantize_loss(0)
+        spend(0)
+        loss(1)
+        quantize_loss(1)
+
+        for step in range(1, TILES - 2):
+            if step == 1:
+                turn_ratings([4], nc.scalar.copy)
+            else:
+                turn(step - 2, step + 3, nc.scalar.copy)
+            score(step + 2)
+            spend(step)
+            weigh(step - 1, 3)
+            loss(step + 1)
+            if live(step + 3):
+                quantize_ratings(step + 3)
+            if live(step - 2):
+                quantize_result(step - 2)
+            quantize_loss(step + 1)
+
+        last = TILES - 1
+        turn(last - 3, -1, nc.scalar.copy)
+        spend(last - 1)
+        loss(last)
+        quantize_result(last - 3)
+        quantize_loss(last)
+        spend(last)
+        weigh(last - 2, 3)
+        weigh(last - 1, 2)
+        turn(last - 2, -1, nc.scalar.copy)
+        cast_on_scalar(last - 1, PIECES[2], PIECES[3])
+        new_result(last)
+        weigh_piece(last, 0, HALF)
+        store_result(last, 0, HALF)
+        weigh_piece(last, HALF, B)
+        store_result(last, HALF, B)
+        turn(last - 1, -1, nc.scalar.copy)
+        cast_on_vector(last, 0, HALF)
+        cast_on_vector(last, HALF, B)
+        quantize_result(last - 2)
+        quantize_result(last - 1)
+        turn(last, -1, nc.vector.tensor_copy)
+        quantize_result(last)

@@ -22,12 +22,14 @@ TILES = S // P
 FG = F // KP
 BG = B // KP
 RING = 6
+SHARED = 4
+OWN = 2
 HALF = B // 2
 PIECES = (0, 256, 768, 1536)
 LAST_PIECES = (0, 512, 768, 1024, 1536)
-R_LOADS = (2, 2, 4, 4, 4)
-WORD_STORES = (4, 4, 4, 1, 1, 1, 1)
-SCALE_STORES = (4, 4, 4, 3, 1)
+R_LOADS = (1, 2, 3, 4, 6)
+WORD_STORES = (4, 4, 2, 2, 2, 1, 1)
+SCALE_STORES = (8, 4, 4)
 
 
 def runs(sizes):
@@ -71,7 +73,6 @@ def tile_supplier_quadratic_loss_h1_kernel(
         nc.gpsimd.dma_start(out=rows[4:8, 0:384], in_=priorities.rearrange("(r n) -> r n", r=4))
         nc.vector.tensor_copy(out=ident_bf16[:], in_=ident_f32[:])
         nc.vector.memset(p_scales[:].rearrange("p g n -> p (g n)").bitcast(I32), 0)
-        nc.scalar.activation(out=warm[:], in_=ident_f32[:, 0:1], func=ACT.Ln, bias=1.0)
 
         r_run = runs(R_LOADS)
         r_tiles = {}
@@ -89,23 +90,25 @@ def tile_supplier_quadratic_loss_h1_kernel(
             cols = slice(2 * KP * g, 2 * KP * (g + 1))
             nc.sync.dma_start(out=w_raw[:, cols].bitcast(I32), in_=criterion_words[0, :, cols].bitcast(I32))
 
-        load_w_words(0)
         load_ratings(0)
+        load_w_words(0)
         for q in range(4):
             nc.sync.dma_start(
                 out=w_scale_raw[32 * q : 32 * q + 4, :].bitcast(I32),
                 in_=criterion_scales[0, 4 * q : 4 * q + 4, :].bitcast(I32),
             )
+        nc.scalar.activation(out=warm[:], in_=ident_f32[:, 0:1], func=ACT.Ln, bias=1.0)
         load_w_words(1)
         load_ratings(1)
-        nc.sync.dma_start(out=p_codes[:, 0, :].bitcast(I32), in_=spend_words[0].bitcast(I32))
+        load_ratings(2)
         for q in range(4):
             nc.sync.dma_start(
                 out=p_scales[32 * q : 32 * q + 4, :, :].bitcast(I32),
                 in_=spend_scales[:, 4 * q : 4 * q + 4, :].rearrange("g r n -> r g n").bitcast(I32),
             )
+        nc.sync.dma_start(out=p_codes[:, 0, :].bitcast(I32), in_=spend_words[0].bitcast(I32))
         nc.sync.dma_start(out=p_codes[:, 1, :].bitcast(I32), in_=spend_words[1].bitcast(I32))
-        for number in range(2, len(R_LOADS)):
+        for number in range(3, len(R_LOADS)):
             load_ratings(number)
 
         def order_w_columns(g):
@@ -118,23 +121,30 @@ def tile_supplier_quadratic_loss_h1_kernel(
                 in_=w_scale_raw[:, KP * g : KP * (g + 1)].rearrange("p (m t) -> p t m", t=4),
             )
 
-        banks_used = []
+        free_banks = ["bank%d" % n for n in range(RING)]
+        bank_tags = {}
 
-        def next_bank():
-            tag = "bank%d" % (len(banks_used) % RING)
-            banks_used.append(tag)
-            return psum.tile([P, KP], F32, name=tag, tag=tag)
+        def next_bank(key):
+            tag = free_banks.pop(0)
+            bank_tags[key] = (tag, psum.tile([P, KP], F32, name=tag, tag=tag))
+            return bank_tags[key][1]
+
+        def release_bank(key):
+            tag, bank = bank_tags[key]
+            free_banks.append(tag)
+            return bank
 
         word_run = runs(WORD_STORES)
         scale_run = runs(SCALE_STORES)
         word_tiles = {}
         scale_tiles = {}
-        r_q, squares, h_q, logs, y_bf16, turned = {}, {}, {}, {}, {}, {}
+        r_q, squares, h_q, h_bf16 = {}, {}, {}, {}
 
         def live(i):
             return 0 <= i < TILES
 
         r_turned, y_turned = {}, {}
+        shared = [keep.tile([P, 4 * 2 * P], F32, name="shared%d" % n, align_bytes=64) for n in range(SHARED)]
 
         def transpose_ratings(bank, half, i):
             number, first, size = r_run[i]
@@ -144,10 +154,10 @@ def tile_supplier_quadratic_loss_h1_kernel(
                 nc.tensor.transpose(bank[:, col : col + P], r_words[:, u : 2 * P : 2], ident_f32[:])
 
         def transpose_result(bank, half, i, g):
-            y_words = y_bf16[i][:].bitcast(F32)
+            y_words = y_bf16[i].bitcast(F32)
             for u in range(2):
                 col = P * (2 * half + u)
-                first = u * (B // 4) + P * g
+                first = u * (B // 4) + P * g if i < TILES - OWN else P * (2 * g + u)
                 nc.tensor.transpose(bank[:, col : col + P], y_words[:, first : first + P], ident_f32[:])
 
         def halves(bank):
@@ -158,64 +168,87 @@ def tile_supplier_quadratic_loss_h1_kernel(
 
         def turn_ratings(tiles, copy):
             slots = work.tile([P, len(tiles), P, 2], F32, tag="r_turned", name="r_turned", align_bytes=64)
-            bank = next_bank()
+            bank = next_bank("r")
             for half, i in enumerate(tiles):
                 transpose_ratings(bank, half, i)
                 r_turned[i] = as_bf16(slots[:, half])
-            copy(out=slots[:], in_=halves(bank)[:, 0 : len(tiles)])
+            copy(out=slots[:], in_=halves(release_bank("r"))[:, 0 : len(tiles)])
 
         def turn(y_tile, r_tile, copy_last):
-            slots = work.tile([P, 4, P, 2], F32, tag="turned", name="turned", align_bytes=64)
+            slots = shared[y_tile % SHARED][:].rearrange("p (n s u) -> p n s u", n=4, u=2)
             y_turned[y_tile] = [as_bf16(slots[:, g]) for g in range(BG)]
-            bank_x = next_bank()
+            bank_x = next_bank("x")
             transpose_result(bank_x, 0, y_tile, 0)
             transpose_result(bank_x, 1, y_tile, 1)
-            bank_y = next_bank()
+            bank_y = next_bank("y")
             transpose_result(bank_y, 0, y_tile, 2)
             used = 1
             if live(r_tile):
                 transpose_ratings(bank_y, 1, r_tile)
                 r_turned[r_tile] = as_bf16(slots[:, 3])
                 used = 2
-            nc.scalar.copy(out=slots[:, 0:2], in_=halves(bank_x))
-            copy_last(out=slots[:, 2 : 2 + used], in_=halves(bank_y)[:, 0:used])
+            copy_last(out=slots[:, 2 : 2 + used], in_=halves(release_bank("y"))[:, 0:used])
+            nc.scalar.copy(out=slots[:, 0:2], in_=halves(release_bank("x")))
 
-        def score(i):
+        def turn_groups(i, groups, copy):
+            slots = shared[i % SHARED][:].rearrange("p (n s u) -> p n s u", n=4, u=2)
+            y_turned[i] = [as_bf16(slots[:, g]) for g in range(BG)]
+            bank = next_bank("y")
+            for half, g in enumerate(groups):
+                transpose_result(bank, half, i, g)
+            copy(out=slots[:, groups[0] : groups[-1] + 1], in_=halves(release_bank("y"))[:, 0 : len(groups)])
+
+        def spend_and_log(i, n):
+            spend(i, n)
+            log(i, n)
+
+        def score_square(i, g):
+            score(i, g)
+            square(i, g)
+
+        def score(i, g):
             codes, scales = r_q[i]
-            squares[i] = work.tile([P, FG, P, 4], F32, tag="squares", name="squares", bufs=3, align_bytes=64)
-            for g in range(FG):
-                bank = next_bank()
-                for t in range(4):
-                    col = KP * g + P * t
-                    nc.tensor.matmul_mx(
-                        out=bank[:, P * t : P * (t + 1)],
-                        lhsT=w_codes[:, 2 * col : 2 * (col + P)].bitcast(FP4X4),
-                        lhsT_scale=w_scales[:, col : col + P],
-                        rhs=codes[:].bitcast(FP8X4),
-                        rhs_scale=scales[:],
-                        start=True,
-                        stop=True,
-                    )
-                nc.scalar.activation(
-                    out=squares[i][:, g], in_=bank[:].rearrange("p (t s) -> p s t", t=4), func=ACT.Square
+            bank = next_bank(("score", i, g))
+            for t in range(4):
+                col = KP * g + P * t
+                nc.tensor.matmul_mx(
+                    out=bank[:, P * t : P * (t + 1)],
+                    lhsT=w_codes[:, 2 * col : 2 * (col + P)].bitcast(FP4X4),
+                    lhsT_scale=w_scales[:, col : col + P],
+                    rhs=codes[:].bitcast(FP8X4),
+                    rhs_scale=scales[:],
+                    start=True,
+                    stop=True,
                 )
 
-        def spend(i):
+        def square(i, g):
+            if i not in squares:
+                squares[i] = work.tile([P, FG, P, 4], F32, tag="squares", name="squares", bufs=4, align_bytes=64)
+            bank = release_bank(("score", i, g))
+            nc.scalar.activation(out=squares[i][:, g], in_=bank[:].rearrange("p (t s) -> p s t", t=4), func=ACT.Square)
+
+        def spend(i, n):
             codes, scales = h_q[i]
-            logs[i] = work.tile([P, B], F32, tag="logs", name="logs", bufs=3, align_bytes=64)
-            for n in range(BG):
-                bank = next_bank()
-                for g in range(FG):
-                    nc.tensor.matmul_mx(
-                        out=bank[:],
-                        lhsT=codes[:, P * g : P * (g + 1)].bitcast(FP8X4),
-                        lhsT_scale=scales[:, P * g : P * (g + 1)],
-                        rhs=p_codes[:, g, 2 * KP * n : 2 * KP * (n + 1)].bitcast(FP4X4),
-                        rhs_scale=p_scales[:, g, KP * n : KP * (n + 1)],
-                        start=(g == 0),
-                        stop=(g == FG - 1),
-                    )
-                nc.scalar.activation(out=logs[i][:, KP * n : KP * (n + 1)], in_=bank[:], func=ACT.Ln, bias=1.0)
+            bank = next_bank(("spend", i, n))
+            for g in range(FG):
+                nc.tensor.matmul_mx(
+                    out=bank[:],
+                    lhsT=codes[:, P * g : P * (g + 1)].bitcast(FP8X4),
+                    lhsT_scale=scales[:, P * g : P * (g + 1)],
+                    rhs=p_codes[:, g, 2 * KP * n : 2 * KP * (n + 1)].bitcast(FP4X4),
+                    rhs_scale=p_scales[:, g, KP * n : KP * (n + 1)],
+                    start=(g == 0),
+                    stop=(g == FG - 1),
+                )
+
+        def log(i, n):
+            bank = release_bank(("spend", i, n))
+            nc.scalar.activation(out=y_f32[i][:, KP * n : KP * (n + 1)], in_=bank[:], func=ACT.Ln, bias=1.0)
+
+        def score_and_square(i):
+            for g in range(FG):
+                score(i, g)
+                square(i, g)
 
         def b_row(lo, hi):
             return const_a[:, lo:hi] if hi <= HALF else const_b[:, lo - HALF : hi - HALF]
@@ -224,10 +257,17 @@ def tile_supplier_quadratic_loss_h1_kernel(
             const_a[:, HALF : HALF + 4 * FG].rearrange("p (t g) -> p g t", t=4).unsqueeze(2).to_broadcast([P, FG, P, 4])
         )
 
-        y_f32 = {}
+        y_f32 = [keep.tile([P, B], F32, name="y%d" % i, align_bytes=64) for i in range(TILES)]
+        y_bf16 = [shared[(i - 2) % SHARED][:].bitcast(BF16)[:, 0:B] for i in range(TILES - OWN)]
+        for i in range(TILES - OWN, TILES):
+            own = keep.tile([P, B], BF16, name="y_bf16_%d" % i, align_bytes=64)
+            y_bf16.append(own[:])
 
         def cast_views(i, lo, hi):
-            out = y_bf16[i][:].rearrange("p (u m e) -> p u m e", u=2, e=2)[:, :, lo // 4 : hi // 4]
+            if i < TILES - OWN:
+                out = y_bf16[i].rearrange("p (u m e) -> p u m e", u=2, e=2)[:, :, lo // 4 : hi // 4]
+            else:
+                out = y_bf16[i][:, lo:hi].rearrange("p (u m e) -> p u m e", u=2, e=2)
             return out, y_f32[i][:, lo:hi].rearrange("p (m u e) -> p u m e", u=2, e=2)
 
         def cast_on_gpsimd(i, lo, hi):
@@ -242,29 +282,19 @@ def tile_supplier_quadratic_loss_h1_kernel(
             out, in_ = cast_views(i, lo, hi)
             nc.scalar.copy(out=out, in_=in_)
 
-        def new_result(i):
-            y_f32[i] = work.tile([P, B], F32, tag="y", name="y", bufs=4, align_bytes=64)
-            y_bf16[i] = work.tile([P, B], BF16, tag="y_bf16", name="y_bf16", align_bytes=64)
-
         def weigh_piece(i, lo, hi):
-            nc.vector.tensor_tensor(out=y_f32[i][:, lo:hi], in0=logs[i][:, lo:hi], in1=b_row(lo, hi), op=ALU.mult)
+            nc.vector.tensor_tensor(out=y_f32[i][:, lo:hi], in0=y_f32[i][:, lo:hi], in1=b_row(lo, hi), op=ALU.mult)
 
         def store_result(i, lo, hi):
             nc.sync.dma_start(out=out_0[P * i : P * (i + 1), lo:hi], in_=y_f32[i][:, lo:hi])
 
-        def weigh(i, gpsimd_pieces):
-            new_result(i)
-            for n in range(3):
-                weigh_piece(i, PIECES[n], PIECES[n + 1])
-                if n < gpsimd_pieces:
-                    cast_on_gpsimd(i, PIECES[n], PIECES[n + 1])
-            store_result(i, 0, B)
-
-        h_bf16 = {}
 
         def loss(i):
-            h_bf16[i] = work.tile([P, FG, P, 4], BF16, tag="h_bf16", name="h_bf16", align_bytes=64)
-            nc.vector.tensor_tensor(out=h_bf16[i][:], in0=squares[i][:], in1=c_view, op=ALU.mult)
+            if i in (2, 3):
+                h_bf16[i] = shared[i % SHARED][:].bitcast(BF16)[:, 0:F].rearrange("p (g s t) -> p g s t", g=FG, t=4)
+            else:
+                h_bf16[i] = work.tile([P, FG, P, 4], BF16, tag="h_bf16", name="h_bf16", align_bytes=64)[:]
+            nc.vector.tensor_tensor(out=h_bf16[i], in0=squares[i][:], in1=c_view, op=ALU.mult)
 
         def quantize_ratings(i):
             codes = work.tile([P, P], U32, tag="r_codes", name="r_codes", bufs=4, align_bytes=64)
@@ -273,47 +303,60 @@ def tile_supplier_quadratic_loss_h1_kernel(
             nc.vector.quantize_mx(out=codes[:].bitcast(FP8X4), scales=scales[:], in_=r_turned[i])
 
         def quantize_loss(i):
-            codes = work.tile([P, FG * P], U32, tag="h_codes", name="h_codes", align_bytes=64)
-            scales = work.tile([P, FG * P], U8, tag="h_scales", name="h_scales", align_bytes=64)
+            codes = work.tile([P, FG * P], U32, tag="h_codes", name="h_codes", bufs=4, align_bytes=64)
+            scales = work.tile([P, FG * P], U8, tag="h_scales", name="h_scales", bufs=4, align_bytes=64)
             h_q[i] = (codes, scales)
             nc.vector.quantize_mx(
-                out=codes[:].bitcast(FP8X4), scales=scales[:], in_=h_bf16[i][:].rearrange("p g s t -> p (g s t)")
+                out=codes[:].bitcast(FP8X4), scales=scales[:], in_=h_bf16[i].rearrange("p g s t -> p (g s t)")
             )
 
-        def quantize_result(i):
+        def quantize_result(i, g):
             w_number, w_first, w_size = word_run[i]
             s_number, s_first, s_size = scale_run[i]
-            if i == w_first:
+            if w_number not in word_tiles:
                 word_tiles[w_number] = keep.tile([P, BG, w_size * P], U32, name="y_words%d" % w_number, align_bytes=64)
-            if i == s_first:
+            if s_number not in scale_tiles:
                 scale_tiles[s_number] = keep.tile([P, BG, s_size * P], U8, name="y_scales%d" % s_number, align_bytes=64)
+            nc.vector.quantize_mx(
+                out=word_tiles[w_number][:, g, P * (i - w_first) : P * (i - w_first + 1)].bitcast(FP8X4),
+                scales=scale_tiles[s_number][:, g, P * (i - s_first) : P * (i - s_first + 1)],
+                in_=y_turned[i][g],
+            )
+
+        def store_planes(i):
+            w_number, w_first, w_size = word_run[i]
+            s_number, s_first, s_size = scale_run[i]
             words = word_tiles[w_number]
             scales = scale_tiles[s_number]
-            for g in range(BG):
-                nc.vector.quantize_mx(
-                    out=words[:, g, P * (i - w_first) : P * (i - w_first + 1)].bitcast(FP8X4),
-                    scales=scales[:, g, P * (i - s_first) : P * (i - s_first + 1)],
-                    in_=y_turned[i][g],
-                )
             if i == w_first + w_size - 1:
                 nc.sync.dma_start(
                     out=out_1.rearrange("g p m t -> p g (m t)")[:, :, 4 * P * w_first : 4 * P * (i + 1)].bitcast(I32),
                     in_=words[:].bitcast(I32),
                 )
             if i == s_first + s_size - 1:
+                queue = nc.scalar if i == TILES - 1 else nc.sync
                 for q in range(4):
-                    nc.sync.dma_start(
+                    queue.dma_start(
                         out=out_2[:, 4 * q : 4 * q + 4, P * s_first : P * (i + 1)]
                         .rearrange("g r m -> r g m")
                         .bitcast(I32),
                         in_=scales[32 * q : 32 * q + 4, :, :].bitcast(I32),
                     )
 
-        def turn_vectors():
+        def finish_planes(i):
+            for g in range(BG):
+                quantize_result(i, g)
+            store_planes(i)
+
+        def turn_coefficients():
             for t in range(4):
                 nc.tensor.transpose(const_a[:, HALF + FG * t : HALF + FG * t + P], rows[:, t:KP:4], ident_bf16[:])
+
+        def turn_priorities():
             for m in range(3):
                 nc.tensor.transpose(const_b[:, P * m : P * (m + 1)], rows[:, P * m : P * (m + 1)], ident_bf16[:])
+
+        def keep_priorities():
             nc.vector.tensor_copy(out=b_cols[:], in_=const_b[:, 0 : 3 * P].rearrange("p (m r) -> p m r", m=3)[:, :, 4:8])
 
         def spread_priorities(blocks):
@@ -325,62 +368,99 @@ def tile_supplier_quadratic_loss_h1_kernel(
                     ident_bf16[:],
                 )
 
-        order_w_columns(0)
         turn_ratings([0], nc.scalar.copy)
-        turn_ratings([1], nc.scalar.copy)
-        turn_ratings([2, 3], nc.scalar.copy)
+        order_w_columns(0)
         quantize_ratings(0)
         order_w_columns(1)
-        quantize_ratings(1)
+        turn_ratings([1, 2], nc.vector.tensor_copy)
         quantize_ratings(2)
-        quantize_ratings(3)
-        score(0)
-        score(1)
-        turn_vectors()
+        score_square(0, 0)
+        quantize_ratings(1)
+        score_square(0, 1)
+        turn_coefficients()
+        score_square(1, 1)
+        score_square(1, 0)
+        turn_ratings([3], nc.scalar.copy)
         loss(0)
-        score(2)
+        turn_priorities()
+        keep_priorities()
+        score_square(2, 0)
+        quantize_ratings(3)
         spread_priorities(range(6, 12))
         spread_priorities(range(6))
+        score_square(2, 1)
         quantize_loss(0)
-        spend(0)
         loss(1)
         quantize_loss(1)
 
-        for step in range(1, TILES - 2):
-            if step == 1:
-                turn_ratings([4], nc.scalar.copy)
-            else:
-                turn(step - 2, step + 3, nc.scalar.copy)
-            score(step + 2)
-            spend(step)
-            weigh(step - 1, 3)
-            loss(step + 1)
-            if live(step + 3):
-                quantize_ratings(step + 3)
+        for step in range(TILES - 2):
+            spend(step, 0)
+            spend(step, 1)
+            log(step, 1)
+            log(step, 0)
             if live(step - 2):
-                quantize_result(step - 2)
-            quantize_loss(step + 1)
+                turn(step - 2, step + 4, nc.scalar.copy)
+            else:
+                turn_ratings([step + 4], nc.scalar.copy)
+            spend(step, 2)
+            if live(step + 3):
+                score(step + 3, 0)
+                score(step + 3, 1)
+                square(step + 3, 1)
+                square(step + 3, 0)
+            log(step, 2)
+            if live(step - 1):
+                cast_on_gpsimd(step - 1, 0, HALF)
+                weigh_piece(step - 1, HALF, B)
+                cast_on_gpsimd(step - 1, HALF, B)
+                store_result(step - 1, 0, B)
+            loss(step + 2)
+            weigh_piece(step, 0, HALF)
+            if live(step - 2):
+                quantize_result(step - 2, 0)
+            if live(step + 4):
+                quantize_ratings(step + 4)
+            quantize_loss(step + 2)
+            if live(step - 2):
+                quantize_result(step - 2, 1)
+                quantize_result(step - 2, 2)
+                store_planes(step - 2)
 
         last = TILES - 1
+        cast_on_gpsimd(last - 2, 0, HALF)
+        weigh_piece(last - 2, HALF, B)
+        cast_on_gpsimd(last - 2, HALF, B)
+        store_result(last - 2, 0, B)
+        spend(last - 1, 0)
+        spend(last - 1, 1)
+        log(last - 1, 1)
+        log(last - 1, 0)
         turn(last - 3, -1, nc.scalar.copy)
-        spend(last - 1)
-        loss(last)
-        quantize_result(last - 3)
-        quantize_loss(last)
-        spend(last)
-        weigh(last - 2, 3)
-        weigh(last - 1, 2)
+        spend(last - 1, 2)
+        spend(last, 0)
+        spend(last, 1)
+        log(last - 1, 2)
+        log(last, 1)
+        log(last, 0)
+        spend_and_log(last, 2)
+        weigh_piece(last - 1, 0, HALF)
+        store_result(last - 1, 0, HALF)
+        weigh_piece(last - 1, HALF, B)
+        store_result(last - 1, HALF, B)
+        cast_on_gpsimd(last - 1, 0, KP)
+        cast_on_gpsimd(last - 1, KP, 2 * KP)
         turn(last - 2, -1, nc.scalar.copy)
-        cast_on_scalar(last - 1, PIECES[2], PIECES[3])
-        new_result(last)
+        cast_on_scalar(last - 1, 2 * KP, B)
         weigh_piece(last, 0, HALF)
         store_result(last, 0, HALF)
         weigh_piece(last, HALF, B)
         store_result(last, HALF, B)
+        cast_on_scalar(last, 0, KP)
         turn(last - 1, -1, nc.scalar.copy)
-        cast_on_vector(last, 0, HALF)
-        cast_on_vector(last, HALF, B)
-        quantize_result(last - 2)
-        quantize_result(last - 1)
-        turn(last, -1, nc.vector.tensor_copy)
-        quantize_result(last)
+        finish_planes(last - 3)
+        cast_on_vector(last, KP, 2 * KP)
+        cast_on_vector(last, 2 * KP, B)
+        finish_planes(last - 2)
+        turn(last, -1, nc.scalar.copy)
+        finish_planes(last - 1)
+        finish_planes(last)

@@ -24,6 +24,9 @@ BG = B // KP
 RING = 6
 SHARED = 4
 OWN = 2
+B_ROWS = B // (2 * P)
+C_WORDS = 2 * FG
+R_ON_VECTOR = (7, 9, 11, 13, 15)
 HALF = B // 2
 PIECES = (0, 256, 768, 1536)
 LAST_PIECES = (0, 512, 768, 1024, 1536)
@@ -59,19 +62,19 @@ def tile_supplier_quadratic_loss_h1_kernel(
         p_codes = keep.tile([P, FG, 2 * B], U8, align_bytes=64)
         p_scales = keep.tile([P, FG, B], U8, align_bytes=64)
         rows = keep.tile([P, KP], BF16, align_bytes=64)
-        b_cols = keep.tile([P, 3, 4], BF16, align_bytes=64)
+        b_cols = keep.tile([P, B_ROWS], F32, align_bytes=64)
         ident_f32 = keep.tile([P, P], F32, align_bytes=64)
-        ident_bf16 = keep.tile([P, P], BF16, align_bytes=64)
         warm = keep.tile([P, 1], F32)
-        const_a = psum.tile([P, 2 * KP], BF16, tag="const_a")
-        const_b = psum.tile([P, 2 * KP], BF16, tag="const_b")
+        const_a = psum.tile([P, KP], F32, tag="const_a")
+        const_b = psum.tile([P, KP], F32, tag="const_b")
 
         nc.vector.memset(w_scale_raw[:].bitcast(I32), 0)
         nc.vector.memset(rows[:], 0.0)
         make_identity(nc, ident_f32[:])
-        nc.gpsimd.dma_start(out=rows[0:FG, :], in_=loss_coef.rearrange("(g n) -> g n", g=FG))
-        nc.gpsimd.dma_start(out=rows[4:8, 0:384], in_=priorities.rearrange("(r n) -> r n", r=4))
-        nc.vector.tensor_copy(out=ident_bf16[:], in_=ident_f32[:])
+        c_rows = loss_coef.rearrange("(g n) -> g n", g=FG)
+        nc.gpsimd.dma_start(out=rows[0:4:2, :], in_=c_rows)
+        nc.gpsimd.dma_start(out=rows[1:4:2, 0 : KP - 2], in_=c_rows[:, 2:KP])
+        nc.gpsimd.dma_start(out=rows[4 : 4 + B_ROWS, 0 : 2 * P], in_=priorities.rearrange("(r n) -> r n", r=B_ROWS))
         nc.vector.memset(p_scales[:].rearrange("p g n -> p (g n)").bitcast(I32), 0)
 
         r_run = runs(R_LOADS)
@@ -124,8 +127,8 @@ def tile_supplier_quadratic_loss_h1_kernel(
         free_banks = ["bank%d" % n for n in range(RING)]
         bank_tags = {}
 
-        def next_bank(key):
-            tag = free_banks.pop(0)
+        def next_bank(key, skip=0):
+            tag = free_banks.pop(skip)
             bank_tags[key] = (tag, psum.tile([P, KP], F32, name=tag, tag=tag))
             return bank_tags[key][1]
 
@@ -143,7 +146,7 @@ def tile_supplier_quadratic_loss_h1_kernel(
         def live(i):
             return 0 <= i < TILES
 
-        r_turned, y_turned = {}, {}
+        r_turned, y_turned, pending_r = {}, {}, {}
         shared = [keep.tile([P, 4 * 2 * P], F32, name="shared%d" % n, align_bytes=64) for n in range(SHARED)]
 
         def transpose_ratings(bank, half, i):
@@ -177,9 +180,9 @@ def tile_supplier_quadratic_loss_h1_kernel(
         def turn(y_tile, r_tile, copy_last):
             slots = shared[y_tile % SHARED][:].rearrange("p (n s u) -> p n s u", n=4, u=2)
             y_turned[y_tile] = [as_bf16(slots[:, g]) for g in range(BG)]
-            bank_x = next_bank("x")
-            transpose_result(bank_x, 0, y_tile, 0)
+            bank_x = next_bank("x", 1)
             transpose_result(bank_x, 1, y_tile, 1)
+            transpose_result(bank_x, 0, y_tile, 0)
             bank_y = next_bank("y")
             transpose_result(bank_y, 0, y_tile, 2)
             used = 1
@@ -187,7 +190,11 @@ def tile_supplier_quadratic_loss_h1_kernel(
                 transpose_ratings(bank_y, 1, r_tile)
                 r_turned[r_tile] = as_bf16(slots[:, 3])
                 used = 2
-            copy_last(out=slots[:, 2 : 2 + used], in_=halves(release_bank("y"))[:, 0:used])
+            y_halves = halves(release_bank("y"))
+            if live(r_tile) and r_tile in R_ON_VECTOR:
+                pending_r[r_tile] = (slots[:, 3:4], y_halves[:, 1:2])
+                used = 1
+            copy_last(out=slots[:, 2 : 2 + used], in_=y_halves[:, 0:used])
             nc.scalar.copy(out=slots[:, 0:2], in_=halves(release_bank("x")))
 
         def turn_groups(i, groups, copy):
@@ -227,9 +234,9 @@ def tile_supplier_quadratic_loss_h1_kernel(
             bank = release_bank(("score", i, g))
             nc.scalar.activation(out=squares[i][:, g], in_=bank[:].rearrange("p (t s) -> p s t", t=4), func=ACT.Square)
 
-        def spend(i, n):
+        def spend(i, n, skip=0):
             codes, scales = h_q[i]
-            bank = next_bank(("spend", i, n))
+            bank = next_bank(("spend", i, n), skip)
             for g in range(FG):
                 nc.tensor.matmul_mx(
                     out=bank[:],
@@ -250,11 +257,18 @@ def tile_supplier_quadratic_loss_h1_kernel(
                 score(i, g)
                 square(i, g)
 
+        b_words = [const_a[:, C_WORDS : C_WORDS + HALF // 2], const_b[:, 0 : HALF // 2]]
+
         def b_row(lo, hi):
-            return const_a[:, lo:hi] if hi <= HALF else const_b[:, lo - HALF : hi - HALF]
+            half = lo // HALF
+            return b_words[half].bitcast(BF16)[:, lo - HALF * half : hi - HALF * half]
 
         c_view = (
-            const_a[:, HALF : HALF + 4 * FG].rearrange("p (t g) -> p g t", t=4).unsqueeze(2).to_broadcast([P, FG, P, 4])
+            const_a[:, 0:C_WORDS]
+            .bitcast(BF16)
+            .rearrange("p (g t) -> p g t", t=4)
+            .unsqueeze(2)
+            .to_broadcast([P, FG, P, 4])
         )
 
         y_f32 = [keep.tile([P, B], F32, name="y%d" % i, align_bytes=64) for i in range(TILES)]
@@ -297,8 +311,8 @@ def tile_supplier_quadratic_loss_h1_kernel(
             nc.vector.tensor_tensor(out=h_bf16[i], in0=squares[i][:], in1=c_view, op=ALU.mult)
 
         def quantize_ratings(i):
-            codes = work.tile([P, P], U32, tag="r_codes", name="r_codes", bufs=4, align_bytes=64)
-            scales = work.tile([P, P], U8, tag="r_scales", name="r_scales", bufs=4, align_bytes=64)
+            codes = work.tile([P, P], U32, tag="r_codes", name="r_codes", bufs=5, align_bytes=64)
+            scales = work.tile([P, P], U8, tag="r_scales", name="r_scales", bufs=5, align_bytes=64)
             r_q[i] = (codes, scales)
             nc.vector.quantize_mx(out=codes[:].bitcast(FP8X4), scales=scales[:], in_=r_turned[i])
 
@@ -348,61 +362,60 @@ def tile_supplier_quadratic_loss_h1_kernel(
                 quantize_result(i, g)
             store_planes(i)
 
+        row_words = rows[:].bitcast(F32)
+
         def turn_coefficients():
-            for t in range(4):
-                nc.tensor.transpose(const_a[:, HALF + FG * t : HALF + FG * t + P], rows[:, t:KP:4], ident_bf16[:])
+            nc.tensor.transpose(const_a[:, 0:P], row_words[:, 0 : 2 * P : 2], ident_f32[:])
 
         def turn_priorities():
-            for m in range(3):
-                nc.tensor.transpose(const_b[:, P * m : P * (m + 1)], rows[:, P * m : P * (m + 1)], ident_bf16[:])
+            nc.tensor.transpose(const_b[:, 0:P], row_words[:, 0:P], ident_f32[:])
 
         def keep_priorities():
-            nc.vector.tensor_copy(out=b_cols[:], in_=const_b[:, 0 : 3 * P].rearrange("p (m r) -> p m r", m=3)[:, :, 4:8])
+            nc.vector.tensor_copy(out=b_cols[:], in_=const_b[:, 4 : 4 + B_ROWS])
 
-        def spread_priorities(blocks):
-            for block in blocks:
-                r, m = divmod(block, 3)
+        def spread_priorities(half):
+            for n in range(B_ROWS // 2):
+                r = half * (B_ROWS // 2) + n
                 nc.tensor.transpose(
-                    b_row(P * block, P * (block + 1)),
-                    b_cols[:, m, r : r + 1].to_broadcast([P, P]),
-                    ident_bf16[:],
+                    b_words[half][:, P * n : P * (n + 1)], b_cols[:, r : r + 1].to_broadcast([P, P]), ident_f32[:]
                 )
 
-        turn_ratings([0], nc.scalar.copy)
         order_w_columns(0)
+        turn_ratings([0], nc.scalar.copy)
         quantize_ratings(0)
         order_w_columns(1)
         turn_ratings([1, 2], nc.vector.tensor_copy)
-        quantize_ratings(2)
         score_square(0, 0)
-        quantize_ratings(1)
         score_square(0, 1)
+        quantize_ratings(1)
+        quantize_ratings(2)
+        turn_ratings([3, 4], nc.scalar.copy)
         turn_coefficients()
-        score_square(1, 1)
-        score_square(1, 0)
-        turn_ratings([3], nc.scalar.copy)
-        loss(0)
         turn_priorities()
         keep_priorities()
+        loss(0)
+        score_square(1, 0)
+        score_square(1, 1)
         score_square(2, 0)
-        quantize_ratings(3)
-        spread_priorities(range(6, 12))
-        spread_priorities(range(6))
         score_square(2, 1)
+        quantize_ratings(3)
         quantize_loss(0)
+        spread_priorities(0)
+        spread_priorities(1)
         loss(1)
+        quantize_ratings(4)
         quantize_loss(1)
 
         for step in range(TILES - 2):
-            spend(step, 0)
+            spend(step, 0, 1)
             spend(step, 1)
             log(step, 1)
             log(step, 0)
             if live(step - 2):
-                turn(step - 2, step + 4, nc.scalar.copy)
+                turn(step - 2, step + 5, nc.scalar.copy)
             else:
-                turn_ratings([step + 4], nc.scalar.copy)
-            spend(step, 2)
+                turn_ratings([step + 5], nc.scalar.copy)
+            spend(step, 2, 1)
             if live(step + 3):
                 score(step + 3, 0)
                 score(step + 3, 1)
@@ -415,11 +428,13 @@ def tile_supplier_quadratic_loss_h1_kernel(
                 cast_on_gpsimd(step - 1, HALF, B)
                 store_result(step - 1, 0, B)
             loss(step + 2)
+            if step + 5 in pending_r:
+                nc.vector.tensor_copy(out=pending_r[step + 5][0], in_=pending_r[step + 5][1])
             weigh_piece(step, 0, HALF)
             if live(step - 2):
                 quantize_result(step - 2, 0)
-            if live(step + 4):
-                quantize_ratings(step + 4)
+            if live(step + 5):
+                quantize_ratings(step + 5)
             quantize_loss(step + 2)
             if live(step - 2):
                 quantize_result(step - 2, 1)

@@ -24,13 +24,14 @@ BG = B // KP
 RING = 6
 SHARED = 4
 OWN = 2
-B_ROWS = B // (2 * P)
+B_ROWS = 8
+B_WORDS = B // (2 * B_ROWS)
 C_WORDS = 2 * FG
 R_ON_VECTOR = (7, 9, 11, 13, 15)
 HALF = B // 2
 PIECES = (0, 256, 768, 1536)
 LAST_PIECES = (0, 512, 768, 1024, 1536)
-R_LOADS = (1, 2, 3, 4, 6)
+R_LOADS = (2, 3, 4, 7)
 WORD_STORES = (4, 4, 2, 2, 2, 1, 1)
 SCALE_STORES = (8, 4, 4)
 
@@ -62,6 +63,7 @@ def tile_supplier_quadratic_loss_h1_kernel(
         p_codes = keep.tile([P, FG, 2 * B], U8, align_bytes=64)
         p_scales = keep.tile([P, FG, B], U8, align_bytes=64)
         rows = keep.tile([P, KP], BF16, align_bytes=64)
+        rows_b = keep.tile([P, 2 * P], BF16, align_bytes=64)
         b_cols = keep.tile([P, B_ROWS], F32, align_bytes=64)
         ident_f32 = keep.tile([P, P], F32, align_bytes=64)
         warm = keep.tile([P, 1], F32)
@@ -70,11 +72,8 @@ def tile_supplier_quadratic_loss_h1_kernel(
 
         nc.vector.memset(w_scale_raw[:].bitcast(I32), 0)
         nc.vector.memset(rows[:], 0.0)
+        nc.vector.memset(rows_b[:], 0.0)
         make_identity(nc, ident_f32[:])
-        c_rows = loss_coef.rearrange("(g n) -> g n", g=FG)
-        nc.gpsimd.dma_start(out=rows[0:4:2, :], in_=c_rows)
-        nc.gpsimd.dma_start(out=rows[1:4:2, 0 : KP - 2], in_=c_rows[:, 2:KP])
-        nc.gpsimd.dma_start(out=rows[4 : 4 + B_ROWS, 0 : 2 * P], in_=priorities.rearrange("(r n) -> r n", r=B_ROWS))
         nc.vector.memset(p_scales[:].rearrange("p g n -> p (g n)").bitcast(I32), 0)
 
         r_run = runs(R_LOADS)
@@ -89,29 +88,27 @@ def tile_supplier_quadratic_loss_h1_kernel(
                 in_=ratings[first * P : (first + size) * P, :].rearrange("(j p) c -> p j c", p=P),
             )
 
-        def load_w_words(g):
-            cols = slice(2 * KP * g, 2 * KP * (g + 1))
-            nc.sync.dma_start(out=w_raw[:, cols].bitcast(I32), in_=criterion_words[0, :, cols].bitcast(I32))
-
         load_ratings(0)
-        load_w_words(0)
+        nc.sync.dma_start(out=w_raw[:].bitcast(I32), in_=criterion_words[0].bitcast(I32))
         for q in range(4):
             nc.sync.dma_start(
                 out=w_scale_raw[32 * q : 32 * q + 4, :].bitcast(I32),
                 in_=criterion_scales[0, 4 * q : 4 * q + 4, :].bitcast(I32),
             )
+        c_rows = loss_coef.rearrange("(g n) -> g n", g=FG)
+        nc.sync.dma_start(out=rows[0:4:2, :], in_=c_rows)
+        nc.sync.dma_start(out=rows[1:4:2, 0 : KP - 2], in_=c_rows[:, 2:KP])
         nc.scalar.activation(out=warm[:], in_=ident_f32[:, 0:1], func=ACT.Ln, bias=1.0)
-        load_w_words(1)
         load_ratings(1)
-        load_ratings(2)
+        b_rows = priorities.rearrange("(r n) -> r n", r=B_ROWS)
+        nc.sync.dma_start(out=rows_b[0:B_ROWS, 0 : 2 * B_WORDS], in_=b_rows)
         for q in range(4):
             nc.sync.dma_start(
                 out=p_scales[32 * q : 32 * q + 4, :, :].bitcast(I32),
                 in_=spend_scales[:, 4 * q : 4 * q + 4, :].rearrange("g r n -> r g n").bitcast(I32),
             )
-        nc.sync.dma_start(out=p_codes[:, 0, :].bitcast(I32), in_=spend_words[0].bitcast(I32))
-        nc.sync.dma_start(out=p_codes[:, 1, :].bitcast(I32), in_=spend_words[1].bitcast(I32))
-        for number in range(3, len(R_LOADS)):
+        nc.sync.dma_start(out=p_codes[:].bitcast(I32), in_=spend_words.rearrange("g p n -> p g n").bitcast(I32))
+        for number in range(2, len(R_LOADS)):
             load_ratings(number)
 
         def order_w_columns(g):
@@ -257,7 +254,7 @@ def tile_supplier_quadratic_loss_h1_kernel(
                 score(i, g)
                 square(i, g)
 
-        b_words = [const_a[:, C_WORDS : C_WORDS + HALF // 2], const_b[:, 0 : HALF // 2]]
+        b_words = [const_a[:, C_WORDS:KP], const_b[:]]
 
         def b_row(lo, hi):
             half = lo // HALF
@@ -368,43 +365,44 @@ def tile_supplier_quadratic_loss_h1_kernel(
             nc.tensor.transpose(const_a[:, 0:P], row_words[:, 0 : 2 * P : 2], ident_f32[:])
 
         def turn_priorities():
-            nc.tensor.transpose(const_b[:, 0:P], row_words[:, 0:P], ident_f32[:])
+            nc.tensor.transpose(const_b[:, 0:P], rows_b[:].bitcast(F32), ident_f32[:])
 
         def keep_priorities():
-            nc.vector.tensor_copy(out=b_cols[:], in_=const_b[:, 4 : 4 + B_ROWS])
+            nc.vector.tensor_copy(out=b_cols[:], in_=const_b[:, 0:B_ROWS])
 
         def spread_priorities(half):
             for n in range(B_ROWS // 2):
                 r = half * (B_ROWS // 2) + n
                 nc.tensor.transpose(
-                    b_words[half][:, P * n : P * (n + 1)], b_cols[:, r : r + 1].to_broadcast([P, P]), ident_f32[:]
+                    b_words[half][:, B_WORDS * n : B_WORDS * n + P], b_cols[:, r : r + 1].to_broadcast([P, P]), ident_f32[:]
                 )
 
-        order_w_columns(0)
         turn_ratings([0], nc.scalar.copy)
+        order_w_columns(0)
         quantize_ratings(0)
         order_w_columns(1)
-        turn_ratings([1, 2], nc.vector.tensor_copy)
+        turn_coefficients()
+        turn_ratings([1], nc.scalar.copy)
         score_square(0, 0)
         score_square(0, 1)
+        turn_ratings([2, 3], nc.scalar.copy)
         quantize_ratings(1)
-        quantize_ratings(2)
-        turn_ratings([3, 4], nc.scalar.copy)
-        turn_coefficients()
         turn_priorities()
-        keep_priorities()
-        loss(0)
         score_square(1, 0)
         score_square(1, 1)
-        score_square(2, 0)
-        score_square(2, 1)
+        turn_ratings([4], nc.scalar.copy)
+        keep_priorities()
+        loss(0)
+        spread_priorities(1)
+        quantize_ratings(2)
         quantize_ratings(3)
         quantize_loss(0)
         spread_priorities(0)
-        spread_priorities(1)
         loss(1)
-        quantize_ratings(4)
+        score_square(2, 1)
         quantize_loss(1)
+        score_square(2, 0)
+        quantize_ratings(4)
 
         for step in range(TILES - 2):
             spend(step, 0, 1)

@@ -17,33 +17,35 @@ ACT = mybir.ActivationFunctionType
 ALU = mybir.AluOpType
 
 P = 128
-KP = 512
+PACK = 4
+GROUP = P * PACK
+QUADS = 4
 TILES = S // P
-FG = F // KP
-BG = B // KP
-RING = 6
-SHARED = 4
-OWN = 2
+F_GROUPS = F // GROUP
+B_GROUPS = B // GROUP
+HALF = B // 2
+C_WORDS = 2 * F_GROUPS
 B_ROWS = 8
 B_WORDS = B // (2 * B_ROWS)
-C_WORDS = 2 * FG
-R_ON_VECTOR = (7, 9, 11, 13, 15)
-HALF = B // 2
-PIECES = (0, 256, 768, 1536)
-LAST_PIECES = (0, 512, 768, 1024, 1536)
+WORK_BANKS = 6
+SHARED = 4
+OWN = 2
+R_AHEAD, SCORE_AHEAD, LOSS_AHEAD = 5, 3, 2
+R_ON_VECTOR = range(7, TILES, 2)
 R_LOADS = (2, 3, 4, 7)
 WORD_STORES = (4, 4, 2, 2, 2, 1, 1)
 SCALE_STORES = (8, 4, 4)
 
 
 def runs(sizes):
-    table = {}
-    first = 0
+    table = []
     for number, size in enumerate(sizes):
-        for i in range(first, first + size):
-            table[i] = (number, first, size)
-        first += size
+        table.extend([(number, len(table), size)] * size)
     return table
+
+
+def live(i):
+    return 0 <= i < TILES
 
 
 def tile_supplier_quadratic_loss_h1_kernel(
@@ -60,105 +62,131 @@ def tile_supplier_quadratic_loss_h1_kernel(
         w_scale_raw = keep.tile([P, F], U8, align_bytes=64)
         w_codes = keep.tile([P, 2 * F], U8, align_bytes=64)
         w_scales = keep.tile([P, F], U8, align_bytes=64)
-        p_codes = keep.tile([P, FG, 2 * B], U8, align_bytes=64)
-        p_scales = keep.tile([P, FG, B], U8, align_bytes=64)
-        rows = keep.tile([P, KP], BF16, align_bytes=64)
-        rows_b = keep.tile([P, 2 * P], BF16, align_bytes=64)
+        p_codes = keep.tile([P, F_GROUPS, 2 * B], U8, align_bytes=64)
+        p_scales = keep.tile([P, F_GROUPS, B], U8, align_bytes=64)
+        c_rows = keep.tile([P, GROUP], BF16, align_bytes=64)
+        b_rows = keep.tile([P, 2 * P], BF16, align_bytes=64)
         b_cols = keep.tile([P, B_ROWS], F32, align_bytes=64)
-        ident_f32 = keep.tile([P, P], F32, align_bytes=64)
-        warm = keep.tile([P, 1], F32)
-        const_a = psum.tile([P, KP], F32, tag="const_a")
-        const_b = psum.tile([P, KP], F32, tag="const_b")
+        ident = keep.tile([P, P], F32, align_bytes=64)
+        const_a = psum.tile([P, GROUP], F32, tag="const_a")
+        const_b = psum.tile([P, GROUP], F32, tag="const_b")
 
         nc.vector.memset(w_scale_raw[:].bitcast(I32), 0)
-        nc.vector.memset(rows[:], 0.0)
-        nc.vector.memset(rows_b[:], 0.0)
-        make_identity(nc, ident_f32[:])
+        nc.vector.memset(c_rows[:], 0.0)
+        make_identity(nc, ident[:])
+        nc.scalar.activation(out=b_rows[:].bitcast(F32), in_=ident[:], func=ACT.Ln, bias=1.0, scale=0.0)
         nc.vector.memset(p_scales[:].rearrange("p g n -> p (g n)").bitcast(I32), 0)
 
         r_run = runs(R_LOADS)
-        r_tiles = {}
+        r_in = {}
 
         def load_ratings(number):
             first = sum(R_LOADS[:number])
             size = R_LOADS[number]
-            r_tiles[number] = keep.tile([P, size, C], BF16, name="r_in%d" % number, align_bytes=64)
+            r_in[number] = keep.tile([P, size, C], BF16, name="r_in%d" % number, align_bytes=64)
             nc.sync.dma_start(
-                out=r_tiles[number][:],
+                out=r_in[number][:],
                 in_=ratings[first * P : (first + size) * P, :].rearrange("(j p) c -> p j c", p=P),
             )
 
         load_ratings(0)
         nc.sync.dma_start(out=w_raw[:].bitcast(I32), in_=criterion_words[0].bitcast(I32))
-        for q in range(4):
+        for q in range(QUADS):
             nc.sync.dma_start(
                 out=w_scale_raw[32 * q : 32 * q + 4, :].bitcast(I32),
                 in_=criterion_scales[0, 4 * q : 4 * q + 4, :].bitcast(I32),
             )
-        c_rows = loss_coef.rearrange("(g n) -> g n", g=FG)
-        nc.sync.dma_start(out=rows[0:4:2, :], in_=c_rows)
-        nc.sync.dma_start(out=rows[1:4:2, 0 : KP - 2], in_=c_rows[:, 2:KP])
-        nc.scalar.activation(out=warm[:], in_=ident_f32[:, 0:1], func=ACT.Ln, bias=1.0)
+        c_groups = loss_coef.rearrange("(g n) -> g n", g=F_GROUPS)
+        nc.sync.dma_start(out=c_rows[0:C_WORDS:2, :], in_=c_groups)
+        nc.sync.dma_start(out=c_rows[1:C_WORDS:2, 0 : GROUP - 2], in_=c_groups[:, 2:GROUP])
         load_ratings(1)
-        b_rows = priorities.rearrange("(r n) -> r n", r=B_ROWS)
-        nc.sync.dma_start(out=rows_b[0:B_ROWS, 0 : 2 * B_WORDS], in_=b_rows)
-        for q in range(4):
+        for q in range(QUADS):
             nc.sync.dma_start(
                 out=p_scales[32 * q : 32 * q + 4, :, :].bitcast(I32),
                 in_=spend_scales[:, 4 * q : 4 * q + 4, :].rearrange("g r n -> r g n").bitcast(I32),
             )
+        nc.sync.dma_start(out=b_rows[0:B_ROWS, 0 : 2 * B_WORDS], in_=priorities.rearrange("(r n) -> r n", r=B_ROWS))
         nc.sync.dma_start(out=p_codes[:].bitcast(I32), in_=spend_words.rearrange("g p n -> p g n").bitcast(I32))
         for number in range(2, len(R_LOADS)):
             load_ratings(number)
 
         def order_w_columns(g):
+            code_cols = slice(2 * GROUP * g, 2 * GROUP * (g + 1))
+            scale_cols = slice(GROUP * g, GROUP * (g + 1))
             nc.vector.tensor_copy(
-                out=w_codes[:, 2 * KP * g : 2 * KP * (g + 1)].rearrange("p (t m b) -> p t m b", t=4, b=2),
-                in_=w_raw[:, 2 * KP * g : 2 * KP * (g + 1)].rearrange("p (m t b) -> p t m b", t=4, b=2),
+                out=w_codes[:, code_cols].rearrange("p (t m b) -> p t m b", t=PACK, b=2),
+                in_=w_raw[:, code_cols].rearrange("p (m t b) -> p t m b", t=PACK, b=2),
             )
             nc.vector.tensor_copy(
-                out=w_scales[:, KP * g : KP * (g + 1)].rearrange("p (t m) -> p t m", t=4),
-                in_=w_scale_raw[:, KP * g : KP * (g + 1)].rearrange("p (m t) -> p t m", t=4),
+                out=w_scales[:, scale_cols].rearrange("p (t m) -> p t m", t=PACK),
+                in_=w_scale_raw[:, scale_cols].rearrange("p (m t) -> p t m", t=PACK),
             )
 
-        free_banks = ["bank%d" % n for n in range(RING)]
-        bank_tags = {}
+        def turn_coefficients():
+            nc.tensor.transpose(const_a[:, 0:P], c_rows[:].bitcast(F32)[:, 0 : 2 * P : 2], ident[:])
 
-        def next_bank(key, skip=0):
+        def turn_priorities():
+            nc.tensor.transpose(const_b[:, 0:P], b_rows[:].bitcast(F32), ident[:])
+
+        def keep_priorities():
+            nc.vector.tensor_copy(out=b_cols[:], in_=const_b[:, 0:B_ROWS])
+
+        b_words = [const_a[:, C_WORDS:GROUP], const_b[:]]
+
+        def spread_priorities(half):
+            for n in range(B_ROWS // 2):
+                row = half * (B_ROWS // 2) + n
+                nc.tensor.transpose(
+                    b_words[half][:, B_WORDS * n : B_WORDS * n + P],
+                    b_cols[:, row : row + 1].to_broadcast([P, P]),
+                    ident[:],
+                )
+
+        c_for_tile = (
+            const_a[:, 0:C_WORDS]
+            .bitcast(BF16)
+            .rearrange("p (g t) -> p g t", t=PACK)
+            .unsqueeze(2)
+            .to_broadcast([P, F_GROUPS, P, PACK])
+        )
+
+        free_banks = ["bank%d" % n for n in range(WORK_BANKS)]
+        taken = {}
+
+        def take_bank(key, skip=0):
             tag = free_banks.pop(skip)
-            bank_tags[key] = (tag, psum.tile([P, KP], F32, name=tag, tag=tag))
-            return bank_tags[key][1]
+            taken[key] = (tag, psum.tile([P, GROUP], F32, name=tag, tag=tag))
+            return taken[key][1]
 
-        def release_bank(key):
-            tag, bank = bank_tags[key]
+        def free_bank(key):
+            tag, bank = taken[key]
             free_banks.append(tag)
             return bank
 
-        word_run = runs(WORD_STORES)
-        scale_run = runs(SCALE_STORES)
-        word_tiles = {}
-        scale_tiles = {}
-        r_q, squares, h_q, h_bf16 = {}, {}, {}, {}
-
-        def live(i):
-            return 0 <= i < TILES
-
-        r_turned, y_turned, pending_r = {}, {}, {}
-        shared = [keep.tile([P, 4 * 2 * P], F32, name="shared%d" % n, align_bytes=64) for n in range(SHARED)]
+        y_f32 = [keep.tile([P, B], F32, name="y%d" % i, align_bytes=64) for i in range(TILES)]
+        shared = [keep.tile([P, 2 * GROUP], F32, name="shared%d" % n, align_bytes=64) for n in range(SHARED)]
+        y_bf16 = [shared[(i - 2) % SHARED][:].bitcast(BF16)[:, 0:B] for i in range(TILES - OWN)]
+        for i in range(TILES - OWN, TILES):
+            own = keep.tile([P, B], BF16, name="y_bf16_%d" % i, align_bytes=64)
+            y_bf16.append(own[:])
+        r_turned, y_turned, r_left_in_bank = {}, {}, {}
+        r_quantised, squares, h_bf16, h_quantised = {}, {}, {}, {}
+        word_run, scale_run = runs(WORD_STORES), runs(SCALE_STORES)
+        y_words, y_scales = {}, {}
 
         def transpose_ratings(bank, half, i):
             number, first, size = r_run[i]
-            r_words = r_tiles[number][:, i - first, :].bitcast(F32)
+            words = r_in[number][:, i - first, :].bitcast(F32)
             for u in range(2):
                 col = P * (2 * half + u)
-                nc.tensor.transpose(bank[:, col : col + P], r_words[:, u : 2 * P : 2], ident_f32[:])
+                nc.tensor.transpose(bank[:, col : col + P], words[:, u : 2 * P : 2], ident[:])
 
         def transpose_result(bank, half, i, g):
-            y_words = y_bf16[i].bitcast(F32)
+            words = y_bf16[i].bitcast(F32)
             for u in range(2):
                 col = P * (2 * half + u)
-                first = u * (B // 4) + P * g if i < TILES - OWN else P * (2 * g + u)
-                nc.tensor.transpose(bank[:, col : col + P], y_words[:, first : first + P], ident_f32[:])
+                first = u * (B // PACK) + P * g if i < TILES - OWN else P * (2 * g + u)
+                nc.tensor.transpose(bank[:, col : col + P], words[:, first : first + P], ident[:])
 
         def halves(bank):
             return bank[:].rearrange("p (h u s) -> p h s u", h=2, u=2)
@@ -166,55 +194,44 @@ def tile_supplier_quadratic_loss_h1_kernel(
         def as_bf16(words):
             return words.rearrange("p s u -> p (s u)").bitcast(BF16)
 
-        def turn_ratings(tiles, copy):
+        def turn_ratings(tiles):
             slots = work.tile([P, len(tiles), P, 2], F32, tag="r_turned", name="r_turned", align_bytes=64)
-            bank = next_bank("r")
+            bank = take_bank("r")
             for half, i in enumerate(tiles):
                 transpose_ratings(bank, half, i)
                 r_turned[i] = as_bf16(slots[:, half])
-            copy(out=slots[:], in_=halves(release_bank("r"))[:, 0 : len(tiles)])
+            nc.scalar.copy(out=slots[:], in_=halves(free_bank("r"))[:, 0 : len(tiles)])
 
-        def turn(y_tile, r_tile, copy_last):
+        def turn(y_tile, r_tile=None):
             slots = shared[y_tile % SHARED][:].rearrange("p (n s u) -> p n s u", n=4, u=2)
-            y_turned[y_tile] = [as_bf16(slots[:, g]) for g in range(BG)]
-            bank_x = next_bank("x", 1)
+            y_turned[y_tile] = [as_bf16(slots[:, g]) for g in range(B_GROUPS)]
+            bank_x = take_bank("x", 1)
             transpose_result(bank_x, 1, y_tile, 1)
             transpose_result(bank_x, 0, y_tile, 0)
-            bank_y = next_bank("y")
-            transpose_result(bank_y, 0, y_tile, 2)
-            used = 1
-            if live(r_tile):
-                transpose_ratings(bank_y, 1, r_tile)
+            bank_z = take_bank("z")
+            transpose_result(bank_z, 0, y_tile, 2)
+            for_scalar = 1
+            if r_tile is not None:
+                transpose_ratings(bank_z, 1, r_tile)
                 r_turned[r_tile] = as_bf16(slots[:, 3])
-                used = 2
-            y_halves = halves(release_bank("y"))
-            if live(r_tile) and r_tile in R_ON_VECTOR:
-                pending_r[r_tile] = (slots[:, 3:4], y_halves[:, 1:2])
-                used = 1
-            copy_last(out=slots[:, 2 : 2 + used], in_=y_halves[:, 0:used])
-            nc.scalar.copy(out=slots[:, 0:2], in_=halves(release_bank("x")))
+                if r_tile in R_ON_VECTOR:
+                    r_left_in_bank[r_tile] = (slots[:, 3:4], halves(bank_z)[:, 1:2])
+                else:
+                    for_scalar = 2
+            nc.scalar.copy(out=slots[:, 2 : 2 + for_scalar], in_=halves(free_bank("z"))[:, 0:for_scalar])
+            nc.scalar.copy(out=slots[:, 0:2], in_=halves(free_bank("x")))
 
-        def turn_groups(i, groups, copy):
-            slots = shared[i % SHARED][:].rearrange("p (n s u) -> p n s u", n=4, u=2)
-            y_turned[i] = [as_bf16(slots[:, g]) for g in range(BG)]
-            bank = next_bank("y")
-            for half, g in enumerate(groups):
-                transpose_result(bank, half, i, g)
-            copy(out=slots[:, groups[0] : groups[-1] + 1], in_=halves(release_bank("y"))[:, 0 : len(groups)])
-
-        def spend_and_log(i, n):
-            spend(i, n)
-            log(i, n)
-
-        def score_square(i, g):
-            score(i, g)
-            square(i, g)
+        def quantize_ratings(i):
+            codes = work.tile([P, P], U32, tag="r_codes", name="r_codes", bufs=R_AHEAD, align_bytes=64)
+            scales = work.tile([P, P], U8, tag="r_scales", name="r_scales", bufs=R_AHEAD, align_bytes=64)
+            r_quantised[i] = (codes, scales)
+            nc.vector.quantize_mx(out=codes[:].bitcast(FP8X4), scales=scales[:], in_=r_turned[i])
 
         def score(i, g):
-            codes, scales = r_q[i]
-            bank = next_bank(("score", i, g))
-            for t in range(4):
-                col = KP * g + P * t
+            codes, scales = r_quantised[i]
+            bank = take_bank(("score", i, g))
+            for t in range(PACK):
+                col = GROUP * g + P * t
                 nc.tensor.matmul_mx(
                     out=bank[:, P * t : P * (t + 1)],
                     lhsT=w_codes[:, 2 * col : 2 * (col + P)].bitcast(FP4X4),
@@ -227,170 +244,146 @@ def tile_supplier_quadratic_loss_h1_kernel(
 
         def square(i, g):
             if i not in squares:
-                squares[i] = work.tile([P, FG, P, 4], F32, tag="squares", name="squares", bufs=4, align_bytes=64)
-            bank = release_bank(("score", i, g))
-            nc.scalar.activation(out=squares[i][:, g], in_=bank[:].rearrange("p (t s) -> p s t", t=4), func=ACT.Square)
-
-        def spend(i, n, skip=0):
-            codes, scales = h_q[i]
-            bank = next_bank(("spend", i, n), skip)
-            for g in range(FG):
-                nc.tensor.matmul_mx(
-                    out=bank[:],
-                    lhsT=codes[:, P * g : P * (g + 1)].bitcast(FP8X4),
-                    lhsT_scale=scales[:, P * g : P * (g + 1)],
-                    rhs=p_codes[:, g, 2 * KP * n : 2 * KP * (n + 1)].bitcast(FP4X4),
-                    rhs_scale=p_scales[:, g, KP * n : KP * (n + 1)],
-                    start=(g == 0),
-                    stop=(g == FG - 1),
+                squares[i] = work.tile(
+                    [P, F_GROUPS, P, PACK], F32, tag="squares", name="squares", bufs=SCORE_AHEAD + 1, align_bytes=64
                 )
+            bank = free_bank(("score", i, g))
+            nc.scalar.activation(
+                out=squares[i][:, g], in_=bank[:].rearrange("p (t s) -> p s t", t=PACK), func=ACT.Square
+            )
 
-        def log(i, n):
-            bank = release_bank(("spend", i, n))
-            nc.scalar.activation(out=y_f32[i][:, KP * n : KP * (n + 1)], in_=bank[:], func=ACT.Ln, bias=1.0)
-
-        def score_and_square(i):
-            for g in range(FG):
-                score(i, g)
-                square(i, g)
-
-        b_words = [const_a[:, C_WORDS:KP], const_b[:]]
-
-        def b_row(lo, hi):
-            half = lo // HALF
-            return b_words[half].bitcast(BF16)[:, lo - HALF * half : hi - HALF * half]
-
-        c_view = (
-            const_a[:, 0:C_WORDS]
-            .bitcast(BF16)
-            .rearrange("p (g t) -> p g t", t=4)
-            .unsqueeze(2)
-            .to_broadcast([P, FG, P, 4])
-        )
-
-        y_f32 = [keep.tile([P, B], F32, name="y%d" % i, align_bytes=64) for i in range(TILES)]
-        y_bf16 = [shared[(i - 2) % SHARED][:].bitcast(BF16)[:, 0:B] for i in range(TILES - OWN)]
-        for i in range(TILES - OWN, TILES):
-            own = keep.tile([P, B], BF16, name="y_bf16_%d" % i, align_bytes=64)
-            y_bf16.append(own[:])
-
-        def cast_views(i, lo, hi):
-            if i < TILES - OWN:
-                out = y_bf16[i].rearrange("p (u m e) -> p u m e", u=2, e=2)[:, :, lo // 4 : hi // 4]
-            else:
-                out = y_bf16[i][:, lo:hi].rearrange("p (u m e) -> p u m e", u=2, e=2)
-            return out, y_f32[i][:, lo:hi].rearrange("p (m u e) -> p u m e", u=2, e=2)
-
-        def cast_on_gpsimd(i, lo, hi):
-            out, in_ = cast_views(i, lo, hi)
-            nc.gpsimd.tensor_scalar(out=out, in0=in_, scalar1=1.0, scalar2=1.0, op0=ALU.mult, op1=ALU.mult)
-
-        def cast_on_vector(i, lo, hi):
-            out, in_ = cast_views(i, lo, hi)
-            nc.vector.tensor_copy(out=out, in_=in_)
-
-        def cast_on_scalar(i, lo, hi):
-            out, in_ = cast_views(i, lo, hi)
-            nc.scalar.copy(out=out, in_=in_)
-
-        def weigh_piece(i, lo, hi):
-            nc.vector.tensor_tensor(out=y_f32[i][:, lo:hi], in0=y_f32[i][:, lo:hi], in1=b_row(lo, hi), op=ALU.mult)
-
-        def store_result(i, lo, hi):
-            nc.sync.dma_start(out=out_0[P * i : P * (i + 1), lo:hi], in_=y_f32[i][:, lo:hi])
-
+        def score_and_square(i, g):
+            score(i, g)
+            square(i, g)
 
         def loss(i):
-            if i in (2, 3):
-                h_bf16[i] = shared[i % SHARED][:].bitcast(BF16)[:, 0:F].rearrange("p (g s t) -> p g s t", g=FG, t=4)
+            if i - LOSS_AHEAD in (0, 1):
+                flat = shared[i % SHARED][:].bitcast(BF16)[:, 0:F]
+                h_bf16[i] = flat.rearrange("p (g s t) -> p g s t", g=F_GROUPS, t=PACK)
             else:
-                h_bf16[i] = work.tile([P, FG, P, 4], BF16, tag="h_bf16", name="h_bf16", align_bytes=64)[:]
-            nc.vector.tensor_tensor(out=h_bf16[i], in0=squares[i][:], in1=c_view, op=ALU.mult)
-
-        def quantize_ratings(i):
-            codes = work.tile([P, P], U32, tag="r_codes", name="r_codes", bufs=5, align_bytes=64)
-            scales = work.tile([P, P], U8, tag="r_scales", name="r_scales", bufs=5, align_bytes=64)
-            r_q[i] = (codes, scales)
-            nc.vector.quantize_mx(out=codes[:].bitcast(FP8X4), scales=scales[:], in_=r_turned[i])
+                h_tile = work.tile([P, F_GROUPS, P, PACK], BF16, tag="h_bf16", name="h_bf16", align_bytes=64)
+                h_bf16[i] = h_tile[:]
+            nc.vector.tensor_tensor(out=h_bf16[i], in0=squares[i][:], in1=c_for_tile, op=ALU.mult)
 
         def quantize_loss(i):
-            codes = work.tile([P, FG * P], U32, tag="h_codes", name="h_codes", bufs=4, align_bytes=64)
-            scales = work.tile([P, FG * P], U8, tag="h_scales", name="h_scales", bufs=4, align_bytes=64)
-            h_q[i] = (codes, scales)
+            depth = LOSS_AHEAD + 2
+            codes = work.tile([P, F_GROUPS * P], U32, tag="h_codes", name="h_codes", bufs=depth, align_bytes=64)
+            scales = work.tile([P, F_GROUPS * P], U8, tag="h_scales", name="h_scales", bufs=depth, align_bytes=64)
+            h_quantised[i] = (codes, scales)
             nc.vector.quantize_mx(
                 out=codes[:].bitcast(FP8X4), scales=scales[:], in_=h_bf16[i].rearrange("p g s t -> p (g s t)")
             )
 
+        def spend(i, n, skip=0):
+            codes, scales = h_quantised[i]
+            bank = take_bank(("spend", i, n), skip)
+            for g in range(F_GROUPS):
+                nc.tensor.matmul_mx(
+                    out=bank[:],
+                    lhsT=codes[:, P * g : P * (g + 1)].bitcast(FP8X4),
+                    lhsT_scale=scales[:, P * g : P * (g + 1)],
+                    rhs=p_codes[:, g, 2 * GROUP * n : 2 * GROUP * (n + 1)].bitcast(FP4X4),
+                    rhs_scale=p_scales[:, g, GROUP * n : GROUP * (n + 1)],
+                    start=(g == 0),
+                    stop=(g == F_GROUPS - 1),
+                )
+
+        def log(i, n):
+            bank = free_bank(("spend", i, n))
+            nc.scalar.activation(out=y_f32[i][:, GROUP * n : GROUP * (n + 1)], in_=bank[:], func=ACT.Ln, bias=1.0)
+
+        def spend_and_log_first_two(i):
+            spend(i, 0, 1)
+            spend(i, 1)
+            log(i, 1)
+            log(i, 0)
+
+        def spend_and_log_third(i):
+            spend(i, 2)
+            log(i, 2)
+
+        def weigh(i, half):
+            y_half = y_f32[i][:, HALF * half : HALF * (half + 1)]
+            nc.vector.tensor_tensor(out=y_half, in0=y_half, in1=b_words[half].bitcast(BF16)[:, 0:HALF], op=ALU.mult)
+
+        def store_result(i, half):
+            cols = slice(HALF * half, HALF * (half + 1))
+            nc.sync.dma_start(out=out_0[P * i : P * (i + 1), cols], in_=y_f32[i][:, cols])
+
+        def rounding_views(i, lo, hi):
+            if i < TILES - OWN:
+                out = y_bf16[i].rearrange("p (u m e) -> p u m e", u=2, e=2)[:, :, lo // PACK : hi // PACK]
+            else:
+                out = y_bf16[i][:, lo:hi].rearrange("p (u m e) -> p u m e", u=2, e=2)
+            return out, y_f32[i][:, lo:hi].rearrange("p (m u e) -> p u m e", u=2, e=2)
+
+        def round_on_gpsimd(i, lo, hi):
+            out, in_ = rounding_views(i, lo, hi)
+            nc.gpsimd.tensor_scalar(out=out, in0=in_, scalar1=1.0, scalar2=1.0, op0=ALU.mult, op1=ALU.mult)
+
+        def round_on_vector(i, lo, hi):
+            out, in_ = rounding_views(i, lo, hi)
+            nc.vector.tensor_copy(out=out, in_=in_)
+
+        def round_on_scalar(i, lo, hi):
+            out, in_ = rounding_views(i, lo, hi)
+            nc.scalar.copy(out=out, in_=in_)
+
         def quantize_result(i, g):
             w_number, w_first, w_size = word_run[i]
             s_number, s_first, s_size = scale_run[i]
-            if w_number not in word_tiles:
-                word_tiles[w_number] = keep.tile([P, BG, w_size * P], U32, name="y_words%d" % w_number, align_bytes=64)
-            if s_number not in scale_tiles:
-                scale_tiles[s_number] = keep.tile([P, BG, s_size * P], U8, name="y_scales%d" % s_number, align_bytes=64)
+            if w_number not in y_words:
+                y_words[w_number] = keep.tile(
+                    [P, B_GROUPS, w_size * P], U32, name="y_words%d" % w_number, align_bytes=64
+                )
+            if s_number not in y_scales:
+                y_scales[s_number] = keep.tile(
+                    [P, B_GROUPS, s_size * P], U8, name="y_scales%d" % s_number, align_bytes=64
+                )
             nc.vector.quantize_mx(
-                out=word_tiles[w_number][:, g, P * (i - w_first) : P * (i - w_first + 1)].bitcast(FP8X4),
-                scales=scale_tiles[s_number][:, g, P * (i - s_first) : P * (i - s_first + 1)],
+                out=y_words[w_number][:, g, P * (i - w_first) : P * (i - w_first + 1)].bitcast(FP8X4),
+                scales=y_scales[s_number][:, g, P * (i - s_first) : P * (i - s_first + 1)],
                 in_=y_turned[i][g],
             )
 
         def store_planes(i):
             w_number, w_first, w_size = word_run[i]
             s_number, s_first, s_size = scale_run[i]
-            words = word_tiles[w_number]
-            scales = scale_tiles[s_number]
             if i == w_first + w_size - 1:
+                word_bytes = slice(PACK * P * w_first, PACK * P * (i + 1))
                 nc.sync.dma_start(
-                    out=out_1.rearrange("g p m t -> p g (m t)")[:, :, 4 * P * w_first : 4 * P * (i + 1)].bitcast(I32),
-                    in_=words[:].bitcast(I32),
+                    out=out_1.rearrange("g p m t -> p g (m t)")[:, :, word_bytes].bitcast(I32),
+                    in_=y_words[w_number][:].bitcast(I32),
                 )
             if i == s_first + s_size - 1:
                 queue = nc.scalar if i == TILES - 1 else nc.sync
-                for q in range(4):
+                for q in range(QUADS):
                     queue.dma_start(
                         out=out_2[:, 4 * q : 4 * q + 4, P * s_first : P * (i + 1)]
                         .rearrange("g r m -> r g m")
                         .bitcast(I32),
-                        in_=scales[32 * q : 32 * q + 4, :, :].bitcast(I32),
+                        in_=y_scales[s_number][32 * q : 32 * q + 4, :, :].bitcast(I32),
                     )
 
         def finish_planes(i):
-            for g in range(BG):
+            for g in range(B_GROUPS):
                 quantize_result(i, g)
             store_planes(i)
 
-        row_words = rows[:].bitcast(F32)
-
-        def turn_coefficients():
-            nc.tensor.transpose(const_a[:, 0:P], row_words[:, 0 : 2 * P : 2], ident_f32[:])
-
-        def turn_priorities():
-            nc.tensor.transpose(const_b[:, 0:P], rows_b[:].bitcast(F32), ident_f32[:])
-
-        def keep_priorities():
-            nc.vector.tensor_copy(out=b_cols[:], in_=const_b[:, 0:B_ROWS])
-
-        def spread_priorities(half):
-            for n in range(B_ROWS // 2):
-                r = half * (B_ROWS // 2) + n
-                nc.tensor.transpose(
-                    b_words[half][:, B_WORDS * n : B_WORDS * n + P], b_cols[:, r : r + 1].to_broadcast([P, P]), ident_f32[:]
-                )
-
-        turn_ratings([0], nc.scalar.copy)
+        turn_ratings([0])
         order_w_columns(0)
         quantize_ratings(0)
         order_w_columns(1)
         turn_coefficients()
-        turn_ratings([1], nc.scalar.copy)
-        score_square(0, 0)
-        score_square(0, 1)
-        turn_ratings([2, 3], nc.scalar.copy)
+        turn_ratings([1])
+        score_and_square(0, 0)
+        score_and_square(0, 1)
+        turn_ratings([2, 3])
         quantize_ratings(1)
         turn_priorities()
-        score_square(1, 0)
-        score_square(1, 1)
-        turn_ratings([4], nc.scalar.copy)
+        score_and_square(1, 0)
+        score_and_square(1, 1)
+        turn_ratings([4])
         keep_priorities()
         loss(0)
         spread_priorities(1)
@@ -399,81 +392,73 @@ def tile_supplier_quadratic_loss_h1_kernel(
         quantize_loss(0)
         spread_priorities(0)
         loss(1)
-        score_square(2, 1)
+        score_and_square(2, 1)
         quantize_loss(1)
-        score_square(2, 0)
+        score_and_square(2, 0)
         quantize_ratings(4)
 
-        for step in range(TILES - 2):
-            spend(step, 0, 1)
-            spend(step, 1)
-            log(step, 1)
-            log(step, 0)
-            if live(step - 2):
-                turn(step - 2, step + 5, nc.scalar.copy)
+        for step in range(TILES - LOSS_AHEAD):
+            r_tile, score_tile, loss_tile = step + R_AHEAD, step + SCORE_AHEAD, step + LOSS_AHEAD
+            round_tile, plane_tile = step - 1, step - 2
+            spend_and_log_first_two(step)
+            if live(plane_tile):
+                turn(plane_tile, r_tile if live(r_tile) else None)
             else:
-                turn_ratings([step + 5], nc.scalar.copy)
+                turn_ratings([r_tile])
             spend(step, 2, 1)
-            if live(step + 3):
-                score(step + 3, 0)
-                score(step + 3, 1)
-                square(step + 3, 1)
-                square(step + 3, 0)
+            if live(score_tile):
+                score(score_tile, 0)
+                score(score_tile, 1)
+                square(score_tile, 1)
+                square(score_tile, 0)
             log(step, 2)
-            if live(step - 1):
-                cast_on_gpsimd(step - 1, 0, HALF)
-                weigh_piece(step - 1, HALF, B)
-                cast_on_gpsimd(step - 1, HALF, B)
-                store_result(step - 1, 0, B)
-            loss(step + 2)
-            if step + 5 in pending_r:
-                nc.vector.tensor_copy(out=pending_r[step + 5][0], in_=pending_r[step + 5][1])
-            weigh_piece(step, 0, HALF)
-            if live(step - 2):
-                quantize_result(step - 2, 0)
-            if live(step + 5):
-                quantize_ratings(step + 5)
-            quantize_loss(step + 2)
-            if live(step - 2):
-                quantize_result(step - 2, 1)
-                quantize_result(step - 2, 2)
-                store_planes(step - 2)
+            if live(round_tile):
+                round_on_gpsimd(round_tile, 0, HALF)
+                weigh(round_tile, 1)
+                round_on_gpsimd(round_tile, HALF, B)
+                store_result(round_tile, 1)
+            loss(loss_tile)
+            if r_tile in r_left_in_bank:
+                slot, source = r_left_in_bank[r_tile]
+                nc.vector.tensor_copy(out=slot, in_=source)
+            weigh(step, 0)
+            store_result(step, 0)
+            if live(plane_tile):
+                quantize_result(plane_tile, 0)
+            if live(r_tile):
+                quantize_ratings(r_tile)
+            quantize_loss(loss_tile)
+            if live(plane_tile):
+                quantize_result(plane_tile, 1)
+                quantize_result(plane_tile, 2)
+                store_planes(plane_tile)
 
         last = TILES - 1
-        cast_on_gpsimd(last - 2, 0, HALF)
-        weigh_piece(last - 2, HALF, B)
-        cast_on_gpsimd(last - 2, HALF, B)
-        store_result(last - 2, 0, B)
-        spend(last - 1, 0)
-        spend(last - 1, 1)
-        log(last - 1, 1)
-        log(last - 1, 0)
-        turn(last - 3, -1, nc.scalar.copy)
-        spend(last - 1, 2)
-        spend(last, 0)
-        spend(last, 1)
-        log(last - 1, 2)
-        log(last, 1)
-        log(last, 0)
-        spend_and_log(last, 2)
-        weigh_piece(last - 1, 0, HALF)
-        store_result(last - 1, 0, HALF)
-        weigh_piece(last - 1, HALF, B)
-        store_result(last - 1, HALF, B)
-        cast_on_gpsimd(last - 1, 0, KP)
-        cast_on_gpsimd(last - 1, KP, 2 * KP)
-        turn(last - 2, -1, nc.scalar.copy)
-        cast_on_scalar(last - 1, 2 * KP, B)
-        weigh_piece(last, 0, HALF)
-        store_result(last, 0, HALF)
-        weigh_piece(last, HALF, B)
-        store_result(last, HALF, B)
-        cast_on_scalar(last, 0, KP)
-        turn(last - 1, -1, nc.scalar.copy)
+        round_on_gpsimd(last - 2, 0, HALF)
+        spend_and_log_first_two(last - 1)
+        weigh(last - 2, 1)
+        spend_and_log_third(last - 1)
+        round_on_gpsimd(last - 2, HALF, B)
+        store_result(last - 2, 1)
+        for half in range(2):
+            weigh(last - 1, half)
+            store_result(last - 1, half)
+        turn(last - 3)
+        spend_and_log_first_two(last)
+        spend_and_log_third(last)
+        round_on_gpsimd(last - 1, 0, GROUP)
+        round_on_gpsimd(last - 1, GROUP, 2 * GROUP)
+        turn(last - 2)
+        round_on_scalar(last - 1, 2 * GROUP, B)
+        for half in range(2):
+            weigh(last, half)
+            store_result(last, half)
+        round_on_scalar(last, 0, GROUP)
+        turn(last - 1)
+        round_on_vector(last, GROUP, 2 * GROUP)
         finish_planes(last - 3)
-        cast_on_vector(last, KP, 2 * KP)
-        cast_on_vector(last, 2 * KP, B)
+        round_on_vector(last, 2 * GROUP, B)
         finish_planes(last - 2)
-        turn(last, -1, nc.scalar.copy)
+        turn(last)
         finish_planes(last - 1)
         finish_planes(last)

from contextlib import ExitStack

import concourse.mybir as mybir
from concourse.masks import make_identity

S, C, F, B = 2048, 512, 1024, 1536
FLOPS = 2 * S * C * F + 2 * S * F * B

F32 = mybir.dt.float32
BF16 = mybir.dt.bfloat16
I32 = mybir.dt.int32
U32 = mybir.dt.uint32
U8 = mybir.dt.uint8
FP8X4 = mybir.dt.float8_e4m3fn_x4
FP4X4 = mybir.dt.float4_e2m1fn_x4
ACT = mybir.ActivationFunctionType
ALU = mybir.AluOpType

P = 128
PACK = 4
GROUP = P * PACK
QUADS = 4
TILES = S // P
F_GROUPS = F // GROUP
B_GROUPS = B // GROUP
HALF = B // 2
C_WORDS = 2 * F_GROUPS
B_ROWS = 8
B_WORDS = B // (2 * B_ROWS)
WORK_BANKS = 6
SHARED = 4
OWN = 2
R_AHEAD, SCORE_AHEAD, LOSS_AHEAD = 5, 3, 2
R_ON_VECTOR = range(7, TILES, 2)
R_LOADS = (2, 3, 4, 7)
WORD_STORES = (4, 4, 2, 2, 2, 1, 1)
SCALE_STORES = (8, 4, 4)


def runs(sizes):
    table = []
    for number, size in enumerate(sizes):
        table.extend([(number, len(table), size)] * size)
    return table


def live(i):
    return 0 <= i < TILES


def tile_supplier_quadratic_loss_h1_kernel(
    tc, ratings, criterion_words, criterion_scales, loss_coef, spend_words, spend_scales, priorities, out_0, out_1, out_2
):
    nc = tc.nc
    with ExitStack() as ctx:
        keep = ctx.enter_context(tc.tile_pool(name="keep", bufs=1))
        work = ctx.enter_context(tc.tile_pool(name="work", bufs=3))
        psum = ctx.enter_context(tc.psum_pool(name="psum", bufs=1))
        ctx.enter_context(tc.manual_schedule())

        w_raw = keep.tile([P, 2 * F], U8, align_bytes=64)
        w_scale_raw = keep.tile([P, F], U8, align_bytes=64)
        w_codes = keep.tile([P, 2 * F], U8, align_bytes=64)
        w_scales = keep.tile([P, F], U8, align_bytes=64)
        p_codes = keep.tile([P, F_GROUPS, 2 * B], U8, align_bytes=64)
        p_scales = keep.tile([P, F_GROUPS, B], U8, align_bytes=64)
        c_rows = keep.tile([P, GROUP], BF16, align_bytes=64)
        b_rows = keep.tile([P, 2 * P], BF16, align_bytes=64)
        b_cols = keep.tile([P, B_ROWS], F32, align_bytes=64)
        ident = keep.tile([P, P], F32, align_bytes=64)
        const_a = psum.tile([P, GROUP], F32, tag="const_a")
        const_b = psum.tile([P, GROUP], F32, tag="const_b")

        nc.vector.memset(w_scale_raw[:].bitcast(I32), 0)
        nc.vector.memset(c_rows[:], 0.0)
        make_identity(nc, ident[:])
        nc.scalar.activation(out=b_rows[:].bitcast(F32), in_=ident[:], func=ACT.Ln, bias=1.0, scale=0.0)
        nc.vector.memset(p_scales[:].rearrange("p g n -> p (g n)").bitcast(I32), 0)

        r_run = runs(R_LOADS)
        r_in = {}

        def load_ratings(number):
            first = sum(R_LOADS[:number])
            size = R_LOADS[number]
            r_in[number] = keep.tile([P, size, C], BF16, name="r_in%d" % number, align_bytes=64)
            nc.sync.dma_start(
                out=r_in[number][:],
                in_=ratings[first * P : (first + size) * P, :].rearrange("(j p) c -> p j c", p=P),
            )

        load_ratings(0)
        nc.sync.dma_start(out=w_raw[:].bitcast(I32), in_=criterion_words[0].bitcast(I32))
        for q in range(QUADS):
            nc.sync.dma_start(
                out=w_scale_raw[32 * q : 32 * q + 4, :].bitcast(I32),
                in_=criterion_scales[0, 4 * q : 4 * q + 4, :].bitcast(I32),
            )
        c_groups = loss_coef.rearrange("(g n) -> g n", g=F_GROUPS)
        nc.sync.dma_start(out=c_rows[0:C_WORDS:2, :], in_=c_groups)
        nc.sync.dma_start(out=c_rows[1:C_WORDS:2, 0 : GROUP - 2], in_=c_groups[:, 2:GROUP])
        load_ratings(1)
        for q in range(QUADS):
            nc.sync.dma_start(
                out=p_scales[32 * q : 32 * q + 4, :, :].bitcast(I32),
                in_=spend_scales[:, 4 * q : 4 * q + 4, :].rearrange("g r n -> r g n").bitcast(I32),
            )
        nc.sync.dma_start(out=b_rows[0:B_ROWS, 0 : 2 * B_WORDS], in_=priorities.rearrange("(r n) -> r n", r=B_ROWS))
        nc.sync.dma_start(out=p_codes[:].bitcast(I32), in_=spend_words.rearrange("g p n -> p g n").bitcast(I32))
        for number in range(2, len(R_LOADS)):
            load_ratings(number)

        def order_w_columns(g):
            code_cols = slice(2 * GROUP * g, 2 * GROUP * (g + 1))
            scale_cols = slice(GROUP * g, GROUP * (g + 1))
            nc.vector.tensor_copy(
                out=w_codes[:, code_cols].rearrange("p (t m b) -> p t m b", t=PACK, b=2),
                in_=w_raw[:, code_cols].rearrange("p (m t b) -> p t m b", t=PACK, b=2),
            )
            nc.vector.tensor_copy(
                out=w_scales[:, scale_cols].rearrange("p (t m) -> p t m", t=PACK),
                in_=w_scale_raw[:, scale_cols].rearrange("p (m t) -> p t m", t=PACK),
            )

        def turn_coefficients():
            nc.tensor.transpose(const_a[:, 0:P], c_rows[:].bitcast(F32)[:, 0 : 2 * P : 2], ident[:])

        def turn_priorities():
            nc.tensor.transpose(const_b[:, 0:P], b_rows[:].bitcast(F32), ident[:])

        def keep_priorities():
            nc.vector.tensor_copy(out=b_cols[:], in_=const_b[:, 0:B_ROWS])

        b_words = [const_a[:, C_WORDS:GROUP], const_b[:]]

        def spread_priorities(half):
            for n in range(B_ROWS // 2):
                row = half * (B_ROWS // 2) + n
                nc.tensor.transpose(
                    b_words[half][:, B_WORDS * n : B_WORDS * n + P],
                    b_cols[:, row : row + 1].to_broadcast([P, P]),
                    ident[:],
                )

        c_for_tile = (
            const_a[:, 0:C_WORDS]
            .bitcast(BF16)
            .rearrange("p (g t) -> p g t", t=PACK)
            .unsqueeze(2)
            .to_broadcast([P, F_GROUPS, P, PACK])
        )

        free_banks = ["bank%d" % n for n in range(WORK_BANKS)]
        taken = {}

        def take_bank(key, skip=0):
            tag = free_banks.pop(skip)
            taken[key] = (tag, psum.tile([P, GROUP], F32, name=tag, tag=tag))
            return taken[key][1]

        def free_bank(key):
            tag, bank = taken[key]
            free_banks.append(tag)
            return bank

        y_f32 = [keep.tile([P, B], F32, name="y%d" % i, align_bytes=64) for i in range(TILES)]
        shared = [keep.tile([P, 2 * GROUP], F32, name="shared%d" % n, align_bytes=64) for n in range(SHARED)]
        y_bf16 = [shared[(i - 2) % SHARED][:].bitcast(BF16)[:, 0:B] for i in range(TILES - OWN)]
        for i in range(TILES - OWN, TILES):
            own = keep.tile([P, B], BF16, name="y_bf16_%d" % i, align_bytes=64)
            y_bf16.append(own[:])
        r_turned, y_turned, r_left_in_bank = {}, {}, {}
        r_quantised, squares, h_bf16, h_quantised = {}, {}, {}, {}
        word_run, scale_run = runs(WORD_STORES), runs(SCALE_STORES)
        y_words, y_scales = {}, {}

        def transpose_ratings(bank, half, i):
            number, first, size = r_run[i]
            words = r_in[number][:, i - first, :].bitcast(F32)
            for u in range(2):
                col = P * (2 * half + u)
                nc.tensor.transpose(bank[:, col : col + P], words[:, u : 2 * P : 2], ident[:])

        def transpose_result(bank, half, i, g):
            words = y_bf16[i].bitcast(F32)
            for u in range(2):
                col = P * (2 * half + u)
                first = u * (B // PACK) + P * g if i < TILES - OWN else P * (2 * g + u)
                nc.tensor.transpose(bank[:, col : col + P], words[:, first : first + P], ident[:])

        def halves(bank):
            return bank[:].rearrange("p (h u s) -> p h s u", h=2, u=2)

        def as_bf16(words):
            return words.rearrange("p s u -> p (s u)").bitcast(BF16)

        def turn_ratings(tiles):
            slots = work.tile([P, len(tiles), P, 2], F32, tag="r_turned", name="r_turned", align_bytes=64)
            bank = take_bank("r")
            for half, i in enumerate(tiles):
                transpose_ratings(bank, half, i)
                r_turned[i] = as_bf16(slots[:, half])
            nc.scalar.copy(out=slots[:], in_=halves(free_bank("r"))[:, 0 : len(tiles)])

        def turn(y_tile, r_tile=None):
            slots = shared[y_tile % SHARED][:].rearrange("p (n s u) -> p n s u", n=4, u=2)
            y_turned[y_tile] = [as_bf16(slots[:, g]) for g in range(B_GROUPS)]
            bank_x = take_bank("x", 1)
            transpose_result(bank_x, 1, y_tile, 1)
            transpose_result(bank_x, 0, y_tile, 0)
            bank_z = take_bank("z")
            transpose_result(bank_z, 0, y_tile, 2)
            for_scalar = 1
            if r_tile is not None:
                transpose_ratings(bank_z, 1, r_tile)
                r_turned[r_tile] = as_bf16(slots[:, 3])
                if r_tile in R_ON_VECTOR:
                    r_left_in_bank[r_tile] = (slots[:, 3:4], halves(bank_z)[:, 1:2])
                else:
                    for_scalar = 2
            nc.scalar.copy(out=slots[:, 2 : 2 + for_scalar], in_=halves(free_bank("z"))[:, 0:for_scalar])
            nc.scalar.copy(out=slots[:, 0:2], in_=halves(free_bank("x")))

        def quantize_ratings(i):
            codes = work.tile([P, P], U32, tag="r_codes", name="r_codes", bufs=R_AHEAD, align_bytes=64)
            scales = work.tile([P, P], U8, tag="r_scales", name="r_scales", bufs=R_AHEAD, align_bytes=64)
            r_quantised[i] = (codes, scales)
            nc.vector.quantize_mx(out=codes[:].bitcast(FP8X4), scales=scales[:], in_=r_turned[i])

        def score(i, g):
            codes, scales = r_quantised[i]
            bank = take_bank(("score", i, g))
            for t in range(PACK):
                col = GROUP * g + P * t
                nc.tensor.matmul_mx(
                    out=bank[:, P * t : P * (t + 1)],
                    lhsT=w_codes[:, 2 * col : 2 * (col + P)].bitcast(FP4X4),
                    lhsT_scale=w_scales[:, col : col + P],
                    rhs=codes[:].bitcast(FP8X4),
                    rhs_scale=scales[:],
                    start=True,
                    stop=True,
                )

        def square(i, g):
            if i not in squares:
                squares[i] = work.tile(
                    [P, F_GROUPS, P, PACK], F32, tag="squares", name="squares", bufs=SCORE_AHEAD + 1, align_bytes=64
                )
            bank = free_bank(("score", i, g))
            nc.scalar.activation(
                out=squares[i][:, g], in_=bank[:].rearrange("p (t s) -> p s t", t=PACK), func=ACT.Square
            )

        def score_and_square(i, g):
            score(i, g)
            square(i, g)

        def loss(i):
            if i - LOSS_AHEAD in (0, 1):
                flat = shared[i % SHARED][:].bitcast(BF16)[:, 0:F]
                h_bf16[i] = flat.rearrange("p (g s t) -> p g s t", g=F_GROUPS, t=PACK)
            else:
                h_tile = work.tile([P, F_GROUPS, P, PACK], BF16, tag="h_bf16", name="h_bf16", align_bytes=64)
                h_bf16[i] = h_tile[:]
            nc.vector.tensor_tensor(out=h_bf16[i], in0=squares[i][:], in1=c_for_tile, op=ALU.mult)

        def quantize_loss(i):
            depth = LOSS_AHEAD + 2
            codes = work.tile([P, F_GROUPS * P], U32, tag="h_codes", name="h_codes", bufs=depth, align_bytes=64)
            scales = work.tile([P, F_GROUPS * P], U8, tag="h_scales", name="h_scales", bufs=depth, align_bytes=64)
            h_quantised[i] = (codes, scales)
            nc.vector.quantize_mx(
                out=codes[:].bitcast(FP8X4), scales=scales[:], in_=h_bf16[i].rearrange("p g s t -> p (g s t)")
            )

        def spend(i, n, skip=0):
            codes, scales = h_quantised[i]
            bank = take_bank(("spend", i, n), skip)
            for g in range(F_GROUPS):
                nc.tensor.matmul_mx(
                    out=bank[:],
                    lhsT=codes[:, P * g : P * (g + 1)].bitcast(FP8X4),
                    lhsT_scale=scales[:, P * g : P * (g + 1)],
                    rhs=p_codes[:, g, 2 * GROUP * n : 2 * GROUP * (n + 1)].bitcast(FP4X4),
                    rhs_scale=p_scales[:, g, GROUP * n : GROUP * (n + 1)],
                    start=(g == 0),
                    stop=(g == F_GROUPS - 1),
                )

        def log(i, n):
            bank = free_bank(("spend", i, n))
            nc.scalar.activation(out=y_f32[i][:, GROUP * n : GROUP * (n + 1)], in_=bank[:], func=ACT.Ln, bias=1.0)

        def spend_and_log_first_two(i):
            spend(i, 0, 1)
            spend(i, 1)
            log(i, 1)
            log(i, 0)

        def spend_and_log_third(i):
            spend(i, 2)
            log(i, 2)

        def weigh(i, half):
            y_half = y_f32[i][:, HALF * half : HALF * (half + 1)]
            nc.vector.tensor_tensor(out=y_half, in0=y_half, in1=b_words[half].bitcast(BF16)[:, 0:HALF], op=ALU.mult)

        def store_result(i, half):
            cols = slice(HALF * half, HALF * (half + 1))
            nc.sync.dma_start(out=out_0[P * i : P * (i + 1), cols], in_=y_f32[i][:, cols])

        def rounding_views(i, lo, hi):
            if i < TILES - OWN:
                out = y_bf16[i].rearrange("p (u m e) -> p u m e", u=2, e=2)[:, :, lo // PACK : hi // PACK]
            else:
                out = y_bf16[i][:, lo:hi].rearrange("p (u m e) -> p u m e", u=2, e=2)
            return out, y_f32[i][:, lo:hi].rearrange("p (m u e) -> p u m e", u=2, e=2)

        def round_on_gpsimd(i, lo, hi):
            out, in_ = rounding_views(i, lo, hi)
            nc.gpsimd.tensor_scalar(out=out, in0=in_, scalar1=1.0, scalar2=1.0, op0=ALU.mult, op1=ALU.mult)

        def round_on_vector(i, lo, hi):
            out, in_ = rounding_views(i, lo, hi)
            nc.vector.tensor_copy(out=out, in_=in_)

        def round_on_scalar(i, lo, hi):
            out, in_ = rounding_views(i, lo, hi)
            nc.scalar.copy(out=out, in_=in_)

        def quantize_result(i, g):
            w_number, w_first, w_size = word_run[i]
            s_number, s_first, s_size = scale_run[i]
            if w_number not in y_words:
                y_words[w_number] = keep.tile(
                    [P, B_GROUPS, w_size * P], U32, name="y_words%d" % w_number, align_bytes=64
                )
            if s_number not in y_scales:
                y_scales[s_number] = keep.tile(
                    [P, B_GROUPS, s_size * P], U8, name="y_scales%d" % s_number, align_bytes=64
                )
            nc.vector.quantize_mx(
                out=y_words[w_number][:, g, P * (i - w_first) : P * (i - w_first + 1)].bitcast(FP8X4),
                scales=y_scales[s_number][:, g, P * (i - s_first) : P * (i - s_first + 1)],
                in_=y_turned[i][g],
            )

        def store_planes(i):
            w_number, w_first, w_size = word_run[i]
            s_number, s_first, s_size = scale_run[i]
            if i == w_first + w_size - 1:
                word_bytes = slice(PACK * P * w_first, PACK * P * (i + 1))
                nc.sync.dma_start(
                    out=out_1.rearrange("g p m t -> p g (m t)")[:, :, word_bytes].bitcast(I32),
                    in_=y_words[w_number][:].bitcast(I32),
                )
            if i == s_first + s_size - 1:
                queue = nc.scalar if i == TILES - 1 else nc.sync
                for q in range(QUADS):
                    queue.dma_start(
                        out=out_2[:, 4 * q : 4 * q + 4, P * s_first : P * (i + 1)]
                        .rearrange("g r m -> r g m")
                        .bitcast(I32),
                        in_=y_scales[s_number][32 * q : 32 * q + 4, :, :].bitcast(I32),
                    )

        def finish_planes(i):
            for g in range(B_GROUPS):
                quantize_result(i, g)
            store_planes(i)

        turn_ratings([0])
        order_w_columns(0)
        quantize_ratings(0)
        order_w_columns(1)
        turn_coefficients()
        turn_ratings([1])
        score_and_square(0, 0)
        score_and_square(0, 1)
        turn_ratings([2, 3])
        quantize_ratings(1)
        turn_priorities()
        score_and_square(1, 0)
        score_and_square(1, 1)
        turn_ratings([4])
        keep_priorities()
        loss(0)
        spread_priorities(1)
        quantize_ratings(2)
        quantize_ratings(3)
        quantize_loss(0)
        spread_priorities(0)
        loss(1)
        score_and_square(2, 1)
        quantize_loss(1)
        score_and_square(2, 0)
        quantize_ratings(4)

        for step in range(TILES - LOSS_AHEAD):
            r_tile, score_tile, loss_tile = step + R_AHEAD, step + SCORE_AHEAD, step + LOSS_AHEAD
            round_tile, plane_tile = step - 1, step - 2
            spend_and_log_first_two(step)
            if live(plane_tile):
                turn(plane_tile, r_tile if live(r_tile) else None)
            else:
                turn_ratings([r_tile])
            spend(step, 2, 1)
            if live(score_tile):
                score(score_tile, 0)
                score(score_tile, 1)
                square(score_tile, 1)
                square(score_tile, 0)
            log(step, 2)
            if live(round_tile):
                round_on_gpsimd(round_tile, 0, HALF)
                weigh(round_tile, 1)
                round_on_gpsimd(round_tile, HALF, B)
                store_result(round_tile, 1)
            loss(loss_tile)
            if r_tile in r_left_in_bank:
                slot, source = r_left_in_bank[r_tile]
                nc.vector.tensor_copy(out=slot, in_=source)
            weigh(step, 0)
            store_result(step, 0)
            if live(plane_tile):
                quantize_result(plane_tile, 0)
            if live(r_tile):
                quantize_ratings(r_tile)
            quantize_loss(loss_tile)
            if live(plane_tile):
                quantize_result(plane_tile, 1)
                quantize_result(plane_tile, 2)
                store_planes(plane_tile)

        last = TILES - 1
        round_on_gpsimd(last - 2, 0, HALF)
        spend_and_log_first_two(last - 1)
        weigh(last - 2, 1)
        spend_and_log_third(last - 1)
        round_on_gpsimd(last - 2, HALF, B)
        store_result(last - 2, 1)
        for half in range(2):
            weigh(last - 1, half)
            store_result(last - 1, half)
        turn(last - 3)
        spend_and_log_first_two(last)
        spend_and_log_third(last)
        round_on_gpsimd(last - 1, 0, GROUP)
        round_on_gpsimd(last - 1, GROUP, 2 * GROUP)
        turn(last - 2)
        round_on_scalar(last - 1, 2 * GROUP, B)
        for half in range(2):
            weigh(last, half)
            store_result(last, half)
        round_on_scalar(last, 0, GROUP)
        turn(last - 1)
        round_on_vector(last, GROUP, 2 * GROUP)
        finish_planes(last - 3)
        round_on_vector(last, 2 * GROUP, B)
        finish_planes(last - 2)
        turn(last)
        finish_planes(last - 1)
        finish_planes(last)
